import numpy as np
import ml_dtypes


def mxq(x, axis, fmt="e4m3"):
    dtype, down = {"e4m3": (ml_dtypes.float8_e4m3fn, 7), "e5m2": (ml_dtypes.float8_e5m2, 14)}[fmt]
    v = np.moveaxis(np.asarray(x, np.float32).astype(ml_dtypes.bfloat16).astype(np.float64), axis, -1)
    blocks = v.reshape(v.shape[:-1] + (-1, 32))
    amax = np.abs(blocks).max(-1, keepdims=True)
    byte = np.maximum(np.where(amax > 0, np.frexp(amax)[1] - 1 + 127, 0) - down, 1)
    scale = np.exp2(byte - 127.0)
    codes = (blocks / scale).astype(np.float32).astype(dtype).astype(np.float64)
    return np.moveaxis((codes * scale).reshape(v.shape), -1, axis)


WIDE = False


def mx_kscale(k):
    if not WIDE:
        return np.ones(k)
    levels = np.array([10, -10, 5, -5, 0])
    if k % 512:
        return np.exp2(np.random.permutation(np.resize(levels, k // 32))).repeat(32)
    a = np.empty((k // 512, 16))
    for p in range(k // 512):
        a[p, :8] = np.random.permutation(np.resize(levels, 8))
        for g in range(8):
            far = levels[np.abs(levels - a[p, g]) >= 10]
            a[p, g + 8] = far[np.random.randint(len(far))]
    return np.exp2(a.ravel()).repeat(32)


def f64(x):
    return np.asarray(x).astype(np.float64)


def striped(idx):
    return np.tile(idx.reshape(-1, 16).T, (8, 1)).astype(np.uint16)


def unstriped(offs):
    return offs[:16].T.reshape(-1).astype(np.int64)


E2M1 = np.array([0.0, 0.5, 1.0, 1.5, 2.0, 3.0, 4.0, 6.0, -0.0, -0.5, -1.0, -1.5, -2.0, -3.0, -4.0, -6.0])


def pack_weight(w, fmt):
    k, n = w.shape
    w = f64(np.asarray(w, np.float32).astype(ml_dtypes.bfloat16)).reshape(k // 32, 32, n)
    amax = np.abs(w).max(1)
    if fmt == "e4m3":
        byte = np.frexp(amax)[1] - 1 + 127 - 7
    else:
        mant, ex = np.frexp(amax / 6.0)
        byte = np.where(mant > 0.5, ex, ex - 1) + 127
    byte = np.clip(np.where(amax > 0, byte, 1), 1, 254)
    scaled = (w * np.exp2(127.0 - byte)[:, None, :]).reshape(k, n).astype(np.float32)
    by_word = np.ascontiguousarray(scaled.reshape(k // 512, 128, 4, n).transpose(0, 1, 3, 2))
    if fmt == "e4m3":
        words = by_word.astype(ml_dtypes.float8_e4m3fn).view(np.uint8)
    else:
        c = by_word.astype(ml_dtypes.float4_e2m1fn).view(np.uint8) & 0xF
        words = (c[..., 0::2] | (c[..., 1::2] << 4)).reshape(k // 512, 128, 2 * n)
    return np.ascontiguousarray(words), np.ascontiguousarray(byte.astype(np.uint8).reshape(k // 512, 16, n))


def unpack_weight(words, scales, fmt):
    g, _, n = scales.shape
    words = np.ascontiguousarray(words).reshape(g, 128, n, -1)
    if fmt == "e4m3":
        vals = words.view(ml_dtypes.float8_e4m3fn).astype(np.float64)
    else:
        nib = np.empty((g, 128, n, 4), np.uint8)
        nib[..., 0::2] = words & 0xF
        nib[..., 1::2] = words >> 4
        vals = E2M1[nib]
    vals = vals * np.repeat(np.exp2(scales.astype(np.float64) - 127.0), 8, axis=1)[..., None]
    return vals.transpose(0, 1, 3, 2).reshape(g * 512, n)


def relu(v):
    return np.maximum(v, 0.0)


K, T, E, C, H, N = 512, 768, 2, 256, 512, 256


def by_expert(wq, xq):
    return np.concatenate([wq[e].T @ xq[:, e * C:(e + 1) * C] for e in range(E)], axis=1)


def setup_inputs():
    n = np.random.standard_normal
    s = mx_kscale(K)
    u = mx_kscale(H)
    slot_token = np.random.permutation(T)[:E * C]
    x = pack_weight(n((K, T)) * s[:, None], "e4m3")
    w = pack_weight(n((K, N)) / np.sqrt(K) / s[:, None], "e4m3")
    return {
        "x_words": x[0],
        "x_scales": x[1],
        "w_words": w[0],
        "w_scales": w[1],
        "wa": (n((E, K, H)) / np.sqrt(K) / s[None, :, None] * u).astype(np.float32),
        "wb": (n((E, H, N)) / np.sqrt(H) / u[None, :, None]).astype(np.float32),
        "gate": np.tile(np.random.uniform(0.2, 1.0, E * C), (128, 1)).astype(np.float32),
        "offs": striped(slot_token),
    }


def reference(x_words, x_scales, w_words, w_scales, wa, wb, gate, offs):
    w = unpack_weight(w_words, w_scales, "e4m3")
    waq = mxq(f64(wa), 1, "e4m3")
    wbq = mxq(f64(wb), 1, "e4m3")
    idx = unstriped(offs)
    x = unpack_weight(x_words, x_scales, "e4m3")
    base = w.T @ x
    h = relu(by_expert(waq, x[:, idx]))
    y = by_expert(wbq, mxq(h, 0, "e4m3"))
    c = np.zeros((N, T))
    c[:, idx] = f64(gate[:1]) * y
    return base + c

@@ -1,0 +1,257 @@
+from contextlib import ExitStack
+
+import concourse.mybir as mybir
+
+K, T, E, C, H, N = 512, 768, 2, 256, 512, 256
+FLOPS = 2 * K * N * T + 2 * E * C * (K * H + H * N)
+
+F32 = mybir.dt.float32
+BF16 = mybir.dt.bfloat16
+I32 = mybir.dt.int32
+U32 = mybir.dt.uint32
+U16 = mybir.dt.uint16
+U8 = mybir.dt.uint8
+FP8X4 = mybir.dt.float8_e4m3fn_x4
+ACT = mybir.ActivationFunctionType
+ALU = mybir.AluOpType
+
+P = 128
+PACK = 4
+NB = N // P
+BANK = 512
+
+
+def tile_moe_adp_relu_kernel(
+    tc, x_words, x_scales, w_words, w_scales, wa, wb, gate, offs, out
+):
+    nc = tc.nc
+    with ExitStack() as ctx:
+        sb = ctx.enter_context(tc.tile_pool(name="sb", bufs=1))
+        ps = ctx.enter_context(tc.psum_pool(name="ps", bufs=1))
+
+        def tile(shape, dtype, name, tag=None):
+            return sb.tile(shape, dtype, name=name, tag=tag or name, align_bytes=64)
+
+        offsets = tile([P, E * C // 16], U16, "offsets")
+        xw = tile([P, T], I32, "xw")
+        xs = tile([P, T], U8, "xs")
+        ws = tile([P, N], U8, "ws")
+        g = [tile([P, C], F32, "g%d" % e) for e in range(E)]
+        wa_raw = [tile([P, PACK, H // 2], F32, "wa_raw%d" % c) for c in range(2)]
+        wb_raw = tile([P, PACK, N], F32, "wb_raw")
+        routed = [tile([P, T], F32, "routed%d" % b) for b in range(NB)]
+        banks = [ps.tile([P, BANK], F32, name="bank%d" % i) for i in range(8)]
+
+        nc.gpsimd.memset(xs[:].bitcast(I32), 0)
+        nc.gpsimd.memset(ws[:].bitcast(I32), 0)
+        for b in range(NB):
+            nc.gpsimd.memset(routed[b][:], 0.0)
+
+        def load_scales(plane, rows):
+            by_row = rows[0].bitcast(I32).rearrange("(q r) c -> r q c", r=4)
+            for r in range(4):
+                nc.sync.dma_start(out=plane[r:P:32, :].bitcast(I32), in_=by_row[r])
+
+        def load_wa(e, c):
+            rows = wa[e].rearrange("(p j) c -> p j c", j=PACK)
+            nc.sync.dma_start(out=wa_raw[c][:], in_=rows[:, :, c * (H // 2) : (c + 1) * (H // 2)])
+
+        def load_wb(e):
+            nc.sync.dma_start(out=wb_raw[:], in_=wb[e].rearrange("(p j) n -> p j n", j=PACK))
+
+        def load_gate(e):
+            nc.sync.dma_start(out=g[e][:], in_=gate[:, e * C : (e + 1) * C])
+
+        def listed(first, count):
+            return offsets[:, first // 16 : (first + count) // 16]
+
+        def gather_words(dst, first, count):
+            nc.vector.tensor_copy(dst.bitcast(U32), xw[:].bitcast(U32).indirect(listed(first, count)))
+
+        def gather_scales(dst, first, count):
+            nc.vector.tensor_copy(dst, xs[:].indirect(listed(first, count)))
+
+        def on_vector(dst, src):
+            nc.vector.tensor_copy(dst, src)
+
+        def on_scalar(dst, src):
+            nc.scalar.activation(dst, src, ACT.Copy)
+
+        wa_bf = {(0, u): tile([P, 2, P, PACK], BF16, "wa_bf0%d" % u) for u in range(2)}
+        wa_codes = [tile([P, H], U32, "wa_codes%d" % e) for e in range(E)]
+        wa_scale = [tile([P, H], U8, "wa_scale%d" % e) for e in range(E)]
+        wb_bf = [tile([P, N, PACK], BF16, "wb_bf%d" % e) for e in range(E)]
+        wb_codes = [tile([P, N], U32, "wb_codes%d" % e) for e in range(E)]
+        wb_scale = [tile([P, N], U8, "wb_scale%d" % e) for e in range(E)]
+        h_bf = [[tile([P, P, PACK], BF16, "h_bf%d%d" % (e, s)) for s in range(2)] for e in range(E)]
+        h_codes = [tile([P, C], U32, "h_codes%d" % e) for e in range(E)]
+        h_scale = [tile([P, C], U8, "h_scale%d" % e) for e in range(E)]
+
+        def round_wa(e, c, u, copy):
+            src = wa_raw[c][:].rearrange("p j (m t) -> p m j t", t=PACK)[:, :, :, 2 * u : 2 * u + 2]
+            dst = wa_bf[e, u][:].rearrange("p v m j -> p m j v")[:, 64 * c : 64 * (c + 1)]
+            copy(dst, src)
+
+        def quantise_wa(e, u):
+            cols = slice(2 * u * P, (2 * u + 2) * P)
+            nc.vector.quantize_mx(
+                out=wa_codes[e][:, cols].bitcast(FP8X4),
+                scales=wa_scale[e][:, cols],
+                in_=wa_bf[e, u][:].rearrange("p v m j -> p (v m j)"),
+            )
+
+        def round_wb(e, c0, c1, copy):
+            src = wb_raw[:].rearrange("p j (c i) -> p c j i", i=4)[:, c0:c1]
+            dst = wb_bf[e][:].rearrange("p (c i) j -> p c j i", i=4)[:, c0:c1]
+            copy(dst, src)
+
+        def quantise_wb(e):
+            nc.vector.quantize_mx(
+                out=wb_codes[e][:].bitcast(FP8X4),
+                scales=wb_scale[e][:],
+                in_=wb_bf[e][:].rearrange("p n j -> p (n j)"),
+            )
+
+        def first_layer(e, s):
+            slots = slice(e * C + s * P, e * C + (s + 1) * P)
+            bank = banks[4 * e + s][:].rearrange("p (t s) -> p t s", t=PACK)
+            for t in range(PACK):
+                cols = slice(t * P, (t + 1) * P)
+                nc.tensor.matmul_mx(
+                    bank[:, t, :],
+                    lhsT=wa_codes[e][:, cols].bitcast(FP8X4),
+                    lhsT_scale=wa_scale[e][:, cols],
+                    rhs=gw[:, slots].bitcast(FP8X4),
+                    rhs_scale=gs[:, slots],
+                    start=True,
+                    stop=True,
+                )
+            nc.scalar.activation(h_bf[e][s][:], bank.rearrange("p t s -> p s t"), ACT.Relu)
+
+        def quantise_h(e, s):
+            nc.vector.quantize_mx(
+                out=h_codes[e][:, s * P : (s + 1) * P].bitcast(FP8X4),
+                scales=h_scale[e][:, s * P : (s + 1) * P],
+                in_=h_bf[e][s][:].rearrange("p s t -> p (s t)"),
+            )
+
+        def second_layer(e, s, b, acc):
+            cols = slice(b * P, (b + 1) * P)
+            nc.tensor.matmul_mx(
+                acc,
+                lhsT=wb_codes[e][:, cols].bitcast(FP8X4),
+                lhsT_scale=wb_scale[e][:, cols],
+                rhs=h_codes[e][:, s * P : (s + 1) * P].bitcast(FP8X4),
+                rhs_scale=h_scale[e][:, s * P : (s + 1) * P],
+                start=True,
+                stop=True,
+            )
+
+        def scatter(e, b, first, count, y):
+            nc.vector.tensor_tensor(
+                routed[b][:].indirect(listed(e * C + first, count)), y, g[e][:, first : first + count], ALU.mult
+            )
+
+        def base_pieces(b):
+            return ((banks[b][:], slice(0, BANK)), (banks[3][:, b * C : (b + 1) * C], slice(BANK, T)))
+
+        def frozen_layer(b, piece):
+            cols = slice(b * P, (b + 1) * P)
+            acc, tokens = base_pieces(b)[piece]
+            nc.tensor.matmul_mx(
+                acc,
+                lhsT=ww[:, cols].bitcast(FP8X4),
+                lhsT_scale=ws[:, cols],
+                rhs=xw[:, tokens].bitcast(FP8X4),
+                rhs_scale=xs[:, tokens],
+                start=True,
+                stop=True,
+            )
+
+        result = [tile([P, T], F32, "result%d" % b) for b in range(NB)]
+
+        def finish(b, piece):
+            acc, tokens = base_pieces(b)[piece]
+            nc.vector.tensor_tensor(result[b][:, tokens], acc, routed[b][:, tokens], ALU.add)
+
+        def store(queue, b, tokens):
+            queue.dma_start(out=out[b * P : (b + 1) * P, tokens], in_=result[b][:, tokens])
+
+        y_tile = tile([P, 7, P], F32, "y_tile")
+        quarter = [slice(i * P, (i + 1) * P) for i in range(4)]
+
+        nc.sync.dma_start(offsets[:], offs)
+        load_scales(xs, x_scales)
+        nc.sync.dma_start(out=xw[:], in_=x_words[0].rearrange("p t d -> p (t d)").bitcast(I32))
+        load_wa(0, 0)
+        load_wa(0, 1)
+        load_wb(0)
+        gw = tile([P, E * C], I32, "gw")
+        gs = tile([P, E * C], U8, "gs")
+        gather_words(gw[:], 0, E * C)
+        gather_scales(gs[:], 0, E * C)
+        round_wa(0, 0, 0, on_scalar)
+        round_wa(0, 0, 1, on_scalar)
+        load_wa(1, 0)
+        load_gate(0)
+        round_wa(0, 1, 0, on_vector)
+        round_wa(0, 1, 1, on_scalar)
+        load_wa(1, 1)
+        for u in range(2):
+            quantise_wa(0, u)
+        for s in range(2):
+            first_layer(0, s)
+        round_wb(0, 0, 64, on_vector)
+        quantise_wb(0)
+        ww = tile([P, N], I32, "ww", tag="wb_bf0")
+        nc.sync.dma_start(out=ww[:], in_=w_words[0].rearrange("p n d -> p (n d)").bitcast(I32))
+        load_wb(1)
+        load_scales(ws, w_scales)
+        load_gate(1)
+
+        quantise_h(0, 0)
+        wa_bf[1, 1] = tile([P, 2, P, PACK], BF16, "wa_bf11", tag="h_bf00")
+        for b in range(NB):
+            second_layer(0, 0, b, banks[2][:, quarter[b]])
+        on_scalar(y_tile[:, 0:2, :].rearrange("p s c -> p (s c)"), banks[2][:, :C])
+        quantise_h(0, 1)
+        wa_bf[1, 0] = tile([P, 2, P, PACK], BF16, "wa_bf10", tag="h_bf01")
+        second_layer(0, 1, 0, banks[2][:, quarter[2]])
+        round_wa(1, 0, 1, on_vector)
+        for b in range(NB):
+            scatter(0, b, 0, P, y_tile[:, b, :])
+        round_wa(1, 0, 0, on_scalar)
+        for u in range(2):
+            round_wa(1, 1, u, on_scalar)
+            quantise_wa(1, u)
+        for piece in range(2):
+            for b in range(NB):
+                frozen_layer(b, piece)
+        y_held = wa_raw[1][:, 0, :P]
+        on_scalar(y_held, banks[2][:, quarter[2]])
+        scatter(0, 0, P, P, y_held)
+        round_wb(1, 0, 64, on_scalar)
+        quantise_wb(1)
+        first_layer(1, 0)
+        quantise_h(1, 0)
+        first_layer(1, 1)
+        second_layer(0, 1, 1, banks[4][:, quarter[0]])
+        on_scalar(y_tile[:, 2, :], banks[4][:, quarter[0]])
+        scatter(0, 1, P, P, y_tile[:, 2, :])
+        quantise_h(1, 1)
+        second_layer(1, 0, 0, banks[6][:, quarter[0]])
+        second_layer(1, 0, 1, banks[7][:, quarter[0]])
+        on_scalar(y_tile[:, 3, :], banks[6][:, quarter[0]])
+        scatter(1, 0, 0, P, y_tile[:, 3, :])
+        second_layer(1, 1, 1, banks[7][:, quarter[1]])
+        second_layer(1, 1, 0, banks[6][:, quarter[1]])
+        y_pair = y_tile[:, 5:7, :].rearrange("p s c -> p (s c)")
+        on_scalar(y_pair, banks[7][:, :C])
+        on_scalar(y_tile[:, 4, :], banks[6][:, quarter[1]])
+        scatter(1, 1, 0, C, y_pair)
+        scatter(1, 0, P, P, y_tile[:, 4, :])
+        for b in (1, 0):
+            finish(b, 0)
+            store(nc.sync, b, slice(0, BANK))
+            finish(b, 1)
+            store(nc.scalar, b, slice(BANK, T))

@@ -35,32 +35,26 @@ def tile_moe_adp_relu_kernel(
         offsets = tile([P, E * C // 16], U16, "offsets")
         xw = tile([P, T], I32, "xw")
         xs = tile([P, T], U8, "xs")
-        ws = tile([P, N], U8, "ws")
-        g = [tile([P, C], F32, "g%d" % e) for e in range(E)]
-        wa_raw = [tile([P, PACK, H // 2], F32, "wa_raw%d" % c) for c in range(2)]
-        wb_raw = tile([P, PACK, N], F32, "wb_raw")
+        g = tile([P, E * C], F32, "g")
+        wa_raw = [tile([P, PACK, H], F32, "wa_raw%d" % e) for e in range(E)]
+        wb_raw = [tile([P, PACK, N], F32, "wb_raw%d" % e) for e in range(E)]
         routed = [tile([P, T], F32, "routed%d" % b) for b in range(NB)]
         banks = [ps.tile([P, BANK], F32, name="bank%d" % i) for i in range(8)]
 
         nc.gpsimd.memset(xs[:].bitcast(I32), 0)
-        nc.gpsimd.memset(ws[:].bitcast(I32), 0)
         for b in range(NB):
-            nc.gpsimd.memset(routed[b][:], 0.0)
+            nc.vector.memset(routed[b][:], 0.0)
 
         def load_scales(plane, rows):
             by_row = rows[0].bitcast(I32).rearrange("(q r) c -> r q c", r=4)
             for r in range(4):
                 nc.sync.dma_start(out=plane[r:P:32, :].bitcast(I32), in_=by_row[r])
 
-        def load_wa(e, c):
-            rows = wa[e].rearrange("(p j) c -> p j c", j=PACK)
-            nc.sync.dma_start(out=wa_raw[c][:], in_=rows[:, :, c * (H // 2) : (c + 1) * (H // 2)])
+        def load_wa(e):
+            nc.sync.dma_start(out=wa_raw[e][:], in_=wa[e].rearrange("(p j) c -> p j c", j=PACK))
 
         def load_wb(e):
-            nc.sync.dma_start(out=wb_raw[:], in_=wb[e].rearrange("(p j) n -> p j n", j=PACK))
-
-        def load_gate(e):
-            nc.sync.dma_start(out=g[e][:], in_=gate[:, e * C : (e + 1) * C])
+            nc.sync.dma_start(out=wb_raw[e][:], in_=wb[e].rearrange("(p j) n -> p j n", j=PACK))
 
         def listed(first, count):
             return offsets[:, first // 16 : (first + count) // 16]
@@ -77,19 +71,22 @@ def tile_moe_adp_relu_kernel(
         def on_scalar(dst, src):
             nc.scalar.activation(dst, src, ACT.Copy)
 
-        wa_bf = {(0, u): tile([P, 2, P, PACK], BF16, "wa_bf0%d" % u) for u in range(2)}
+        rounded = tile([P, 2816], BF16, "rounded")
+        wa_bf = [rounded[:, 0:1024], rounded[:, 1024:2048]]
         wa_codes = [tile([P, H], U32, "wa_codes%d" % e) for e in range(E)]
         wa_scale = [tile([P, H], U8, "wa_scale%d" % e) for e in range(E)]
-        wb_bf = [tile([P, N, PACK], BF16, "wb_bf%d" % e) for e in range(E)]
+        wb_bf0 = tile([P, N * PACK], BF16, "wb_bf0")
+        wb_bf = [wb_bf0[:], rounded[:, 1792:2816]]
         wb_codes = [tile([P, N], U32, "wb_codes%d" % e) for e in range(E)]
         wb_scale = [tile([P, N], U8, "wb_scale%d" % e) for e in range(E)]
-        h_bf = [[tile([P, P, PACK], BF16, "h_bf%d%d" % (e, s)) for s in range(2)] for e in range(E)]
+        h_rest = tile([P, 3, P * PACK], BF16, "h_rest")
+        h_bf = [[rounded[:, 768:1280], h_rest[:, 0, :]], [h_rest[:, 1, :], h_rest[:, 2, :]]]
         h_codes = [tile([P, C], U32, "h_codes%d" % e) for e in range(E)]
         h_scale = [tile([P, C], U8, "h_scale%d" % e) for e in range(E)]
 
-        def round_wa(e, c, u, copy):
-            src = wa_raw[c][:].rearrange("p j (m t) -> p m j t", t=PACK)[:, :, :, 2 * u : 2 * u + 2]
-            dst = wa_bf[e, u][:].rearrange("p v m j -> p m j v")[:, 64 * c : 64 * (c + 1)]
+        def round_wa(e, u, m0, m1, copy):
+            src = wa_raw[e][:].rearrange("p j (m t) -> p m j t", t=PACK)[:, m0:m1, :, 2 * u : 2 * u + 2]
+            dst = wa_bf[u].rearrange("p (v m j) -> p m j v", v=2, j=PACK)[:, m0:m1]
             copy(dst, src)
 
         def quantise_wa(e, u):
@@ -97,24 +94,24 @@ def tile_moe_adp_relu_kernel(
             nc.vector.quantize_mx(
                 out=wa_codes[e][:, cols].bitcast(FP8X4),
                 scales=wa_scale[e][:, cols],
-                in_=wa_bf[e, u][:].rearrange("p v m j -> p (v m j)"),
+                in_=wa_bf[u],
             )
 
         def round_wb(e, c0, c1, copy):
-            src = wb_raw[:].rearrange("p j (c i) -> p c j i", i=4)[:, c0:c1]
-            dst = wb_bf[e][:].rearrange("p (c i) j -> p c j i", i=4)[:, c0:c1]
+            src = wb_raw[e][:].rearrange("p j (c i) -> p c j i", i=4)[:, c0:c1]
+            dst = wb_bf[e].rearrange("p (c i j) -> p c j i", i=4, j=PACK)[:, c0:c1]
             copy(dst, src)
 
         def quantise_wb(e):
             nc.vector.quantize_mx(
                 out=wb_codes[e][:].bitcast(FP8X4),
                 scales=wb_scale[e][:],
-                in_=wb_bf[e][:].rearrange("p n j -> p (n j)"),
+                in_=wb_bf[e],
             )
 
         def first_layer(e, s):
             slots = slice(e * C + s * P, e * C + (s + 1) * P)
-            bank = banks[4 * e + s][:].rearrange("p (t s) -> p t s", t=PACK)
+            bank = banks[2 * e + s][:].rearrange("p (t s) -> p t s", t=PACK)
             for t in range(PACK):
                 cols = slice(t * P, (t + 1) * P)
                 nc.tensor.matmul_mx(
@@ -126,34 +123,34 @@ def tile_moe_adp_relu_kernel(
                     start=True,
                     stop=True,
                 )
-            nc.scalar.activation(h_bf[e][s][:], bank.rearrange("p t s -> p s t"), ACT.Relu)
+            nc.scalar.activation(h_bf[e][s].rearrange("p (s t) -> p s t", t=PACK), bank.rearrange("p t s -> p s t"), ACT.Relu)
 
-        def quantise_h(e, s):
+        def quantise_h(e, places, values):
             nc.vector.quantize_mx(
-                out=h_codes[e][:, s * P : (s + 1) * P].bitcast(FP8X4),
-                scales=h_scale[e][:, s * P : (s + 1) * P],
-                in_=h_bf[e][s][:].rearrange("p s t -> p (s t)"),
+                out=h_codes[e][:, places].bitcast(FP8X4),
+                scales=h_scale[e][:, places],
+                in_=values,
             )
 
-        def second_layer(e, s, b, acc):
+        def second_layer(e, b, places, acc):
             cols = slice(b * P, (b + 1) * P)
             nc.tensor.matmul_mx(
                 acc,
                 lhsT=wb_codes[e][:, cols].bitcast(FP8X4),
                 lhsT_scale=wb_scale[e][:, cols],
-                rhs=h_codes[e][:, s * P : (s + 1) * P].bitcast(FP8X4),
-                rhs_scale=h_scale[e][:, s * P : (s + 1) * P],
+                rhs=h_codes[e][:, places].bitcast(FP8X4),
+                rhs_scale=h_scale[e][:, places],
                 start=True,
                 stop=True,
             )
 
         def scatter(e, b, first, count, y):
             nc.vector.tensor_tensor(
-                routed[b][:].indirect(listed(e * C + first, count)), y, g[e][:, first : first + count], ALU.mult
+                routed[b][:].indirect(listed(e * C + first, count)), y, g[:, e * C + first : e * C + first + count], ALU.mult
             )
 
         def base_pieces(b):
-            return ((banks[b][:], slice(0, BANK)), (banks[3][:, b * C : (b + 1) * C], slice(BANK, T)))
+            return ((banks[6 + b][:], slice(0, BANK)), (banks[4][:, b * C : (b + 1) * C], slice(BANK, T)))
 
         def frozen_layer(b, piece):
             cols = slice(b * P, (b + 1) * P)
@@ -177,80 +174,65 @@ def tile_moe_adp_relu_kernel(
         def store(queue, b, tokens):
             queue.dma_start(out=out[b * P : (b + 1) * P, tokens], in_=result[b][:, tokens])
 
-        y_tile = tile([P, 7, P], F32, "y_tile")
-        quarter = [slice(i * P, (i + 1) * P) for i in range(4)]
+        y_tile = tile([P, NB, C], F32, "y_tile")
+        every, lower, upper = slice(0, C), slice(0, P), slice(P, C)
 
         nc.sync.dma_start(offsets[:], offs)
         load_scales(xs, x_scales)
         nc.sync.dma_start(out=xw[:], in_=x_words[0].rearrange("p t d -> p (t d)").bitcast(I32))
-        load_wa(0, 0)
-        load_wa(0, 1)
+        load_wa(0)
         load_wb(0)
+        load_wa(1)
+        nc.sync.dma_start(out=g[:], in_=gate)
+        load_wb(1)
         gw = tile([P, E * C], I32, "gw")
         gs = tile([P, E * C], U8, "gs")
         gather_words(gw[:], 0, E * C)
         gather_scales(gs[:], 0, E * C)
-        round_wa(0, 0, 0, on_scalar)
-        round_wa(0, 0, 1, on_scalar)
-        load_wa(1, 0)
-        load_gate(0)
-        round_wa(0, 1, 0, on_vector)
-        round_wa(0, 1, 1, on_scalar)
-        load_wa(1, 1)
+        round_wa(0, 0, 0, P, on_vector)
+        round_wa(0, 1, 0, 40, on_vector)
+        round_wa(0, 1, 40, P, on_scalar)
         for u in range(2):
             quantise_wa(0, u)
         for s in range(2):
             first_layer(0, s)
         round_wb(0, 0, 64, on_vector)
-        quantise_wb(0)
-        ww = tile([P, N], I32, "ww", tag="wb_bf0")
-        nc.sync.dma_start(out=ww[:], in_=w_words[0].rearrange("p n d -> p (n d)").bitcast(I32))
-        load_wb(1)
+        ws = tile([P, N], U8, "ws", tag="wb_raw0")
         load_scales(ws, w_scales)
-        load_gate(1)
-
-        quantise_h(0, 0)
-        wa_bf[1, 1] = tile([P, 2, P, PACK], BF16, "wa_bf11", tag="h_bf00")
-        for b in range(NB):
-            second_layer(0, 0, b, banks[2][:, quarter[b]])
-        on_scalar(y_tile[:, 0:2, :].rearrange("p s c -> p (s c)"), banks[2][:, :C])
-        quantise_h(0, 1)
-        wa_bf[1, 0] = tile([P, 2, P, PACK], BF16, "wa_bf10", tag="h_bf01")
-        second_layer(0, 1, 0, banks[2][:, quarter[2]])
-        round_wa(1, 0, 1, on_vector)
-        for b in range(NB):
-            scatter(0, b, 0, P, y_tile[:, b, :])
-        round_wa(1, 0, 0, on_scalar)
+        quantise_wb(0)
+        quantise_h(0, lower, h_bf[0][0])
+        quantise_h(0, upper, h_bf[0][1])
+        second_layer(0, 0, every, banks[2][:, every])
+        second_layer(0, 1, lower, banks[3][:, lower])
+        second_layer(0, 1, upper, banks[4][:, lower])
+        ww = tile([P, N], I32, "ww", tag="h_scale0")
+        nc.sync.dma_start(out=ww[:], in_=w_words[0].rearrange("p n d -> p (n d)").bitcast(I32))
+        round_wa(1, 0, 0, P, on_vector)
+        round_wa(1, 1, 0, P, on_scalar)
         for u in range(2):
-            round_wa(1, 1, u, on_scalar)
             quantise_wa(1, u)
-        for piece in range(2):
-            for b in range(NB):
-                frozen_layer(b, piece)
-        y_held = wa_raw[1][:, 0, :P]
-        on_scalar(y_held, banks[2][:, quarter[2]])
-        scatter(0, 0, P, P, y_held)
+        y_held = wa_raw[1][:, 0, every]
+        on_scalar(y_held, banks[2][:, every])
+        y_next = wa_raw[1][:, 1, lower]
+        on_scalar(y_next, banks[3][:, lower])
+        scatter(0, 0, 0, C, y_held)
+        scatter(0, 1, 0, P, y_next)
         round_wb(1, 0, 64, on_scalar)
         quantise_wb(1)
-        first_layer(1, 0)
-        quantise_h(1, 0)
-        first_layer(1, 1)
-        second_layer(0, 1, 1, banks[4][:, quarter[0]])
-        on_scalar(y_tile[:, 2, :], banks[4][:, quarter[0]])
-        scatter(0, 1, P, P, y_tile[:, 2, :])
-        quantise_h(1, 1)
-        second_layer(1, 0, 0, banks[6][:, quarter[0]])
-        second_layer(1, 0, 1, banks[7][:, quarter[0]])
-        on_scalar(y_tile[:, 3, :], banks[6][:, quarter[0]])
-        scatter(1, 0, 0, P, y_tile[:, 3, :])
-        second_layer(1, 1, 1, banks[7][:, quarter[1]])
-        second_layer(1, 1, 0, banks[6][:, quarter[1]])
-        y_pair = y_tile[:, 5:7, :].rearrange("p s c -> p (s c)")
-        on_scalar(y_pair, banks[7][:, :C])
-        on_scalar(y_tile[:, 4, :], banks[6][:, quarter[1]])
-        scatter(1, 1, 0, C, y_pair)
-        scatter(1, 0, P, P, y_tile[:, 4, :])
-        for b in (1, 0):
+        for s in range(2):
+            first_layer(1, s)
+        quantise_h(1, every, h_rest[:, 1:3, :].rearrange("p s c -> p (s c)"))
+        y_late = tile([P, P], F32, "y_late", tag="gw")
+        on_scalar(y_late[:], banks[4][:, lower])
+        scatter(0, 1, P, P, y_late[:])
+        for b in range(NB):
+            second_layer(1, b, every, banks[6 + b][:, every])
+            on_scalar(y_tile[:, b, :], banks[6 + b][:, every])
+            scatter(1, b, 0, C, y_tile[:, b, :])
+        for piece in (1, 0):
+            for b in range(NB):
+                frozen_layer(b, piece)
+        for b in range(NB):
             finish(b, 0)
             store(nc.sync, b, slice(0, BANK))
             finish(b, 1)

@@ -35,35 +35,41 @@ def tile_moe_adp_relu_kernel(
         offsets = tile([P, E * C // 16], U16, "offsets")
         xw = tile([P, T], I32, "xw")
         xs = tile([P, T], U8, "xs")
-        g = tile([P, E * C], F32, "g")
+        ww = tile([P, N], I32, "ww")
+        ws = tile([P, N], U8, "ws")
+        gw = tile([P, E * C], I32, "gw")
+        gs = tile([P, E * C], U8, "gs")
+        g = [tile([P, C], F32, "g%d" % e) for e in range(E)]
         wa_raw = [tile([P, PACK, H], F32, "wa_raw%d" % e) for e in range(E)]
         wb_raw = [tile([P, PACK, N], F32, "wb_raw%d" % e) for e in range(E)]
+        wa_bf = [[tile([P, 2 * P * PACK], BF16, "wa_bf0%d" % u)[:] for u in range(2)]]
+        wb_bf = [tile([P, N * PACK], BF16, "wb_bf%d" % e) for e in range(E)]
+        h_first = [tile([P, P * PACK], BF16, "h_bf0%d" % s) for s in range(2)]
+        h_bf = [[h_first[0][:], h_first[1][:]]]
+        wa_codes = [tile([P, H], U32, "wa_codes%d" % e) for e in range(E)]
+        wa_scale = [tile([P, H], U8, "wa_scale%d" % e) for e in range(E)]
+        wb_codes = [tile([P, N], U32, "wb_codes%d" % e) for e in range(E)]
+        wb_scale = [tile([P, N], U8, "wb_scale%d" % e) for e in range(E)]
+        h_codes = [tile([P, C], U32, "h_codes%d" % e) for e in range(E)]
+        h_scale = [tile([P, C], U8, "h_scale%d" % e) for e in range(E)]
+        y = tile([P, E * NB * C], F32, "y")
         routed = [tile([P, T], F32, "routed%d" % b) for b in range(NB)]
+        result = [tile([P, T], F32, "result%d" % b) for b in range(NB)]
         banks = [ps.tile([P, BANK], F32, name="bank%d" % i) for i in range(8)]
 
-        nc.gpsimd.memset(xs[:].bitcast(I32), 0)
-        for b in range(NB):
-            nc.vector.memset(routed[b][:], 0.0)
-
-        def load_scales(plane, rows):
+        def load_scales(queue, plane, rows):
             by_row = rows[0].bitcast(I32).rearrange("(q r) c -> r q c", r=4)
             for r in range(4):
-                nc.sync.dma_start(out=plane[r:P:32, :].bitcast(I32), in_=by_row[r])
+                queue.dma_start(out=plane[r:P:32, :].bitcast(I32), in_=by_row[r])
 
-        def load_wa(e):
-            nc.sync.dma_start(out=wa_raw[e][:], in_=wa[e].rearrange("(p j) c -> p j c", j=PACK))
+        def load_rows(raw, matrix):
+            nc.sync.dma_start(out=raw[:], in_=matrix.rearrange("(p j) c -> p j c", j=PACK))
 
-        def load_wb(e):
-            nc.sync.dma_start(out=wb_raw[e][:], in_=wb[e].rearrange("(p j) n -> p j n", j=PACK))
+        def load_gate(e):
+            nc.sync.dma_start(out=g[e][:], in_=gate[:, e * C : (e + 1) * C])
 
         def listed(first, count):
             return offsets[:, first // 16 : (first + count) // 16]
-
-        def gather_words(dst, first, count):
-            nc.vector.tensor_copy(dst.bitcast(U32), xw[:].bitcast(U32).indirect(listed(first, count)))
-
-        def gather_scales(dst, first, count):
-            nc.vector.tensor_copy(dst, xs[:].indirect(listed(first, count)))
 
         def on_vector(dst, src):
             nc.vector.tensor_copy(dst, src)
@@ -71,169 +77,136 @@ def tile_moe_adp_relu_kernel(
         def on_scalar(dst, src):
             nc.scalar.activation(dst, src, ACT.Copy)
 
-        rounded = tile([P, 2816], BF16, "rounded")
-        wa_bf = [rounded[:, 0:1024], rounded[:, 1024:2048]]
-        wa_codes = [tile([P, H], U32, "wa_codes%d" % e) for e in range(E)]
-        wa_scale = [tile([P, H], U8, "wa_scale%d" % e) for e in range(E)]
-        wb_bf0 = tile([P, N * PACK], BF16, "wb_bf0")
-        wb_bf = [wb_bf0[:], rounded[:, 1792:2816]]
-        wb_codes = [tile([P, N], U32, "wb_codes%d" % e) for e in range(E)]
-        wb_scale = [tile([P, N], U8, "wb_scale%d" % e) for e in range(E)]
-        h_rest = tile([P, 3, P * PACK], BF16, "h_rest")
-        h_bf = [[rounded[:, 768:1280], h_rest[:, 0, :]], [h_rest[:, 1, :], h_rest[:, 2, :]]]
-        h_codes = [tile([P, C], U32, "h_codes%d" % e) for e in range(E)]
-        h_scale = [tile([P, C], U8, "h_scale%d" % e) for e in range(E)]
-
         def round_wa(e, u, m0, m1, copy):
             src = wa_raw[e][:].rearrange("p j (m t) -> p m j t", t=PACK)[:, m0:m1, :, 2 * u : 2 * u + 2]
-            dst = wa_bf[u].rearrange("p (v m j) -> p m j v", v=2, j=PACK)[:, m0:m1]
+            dst = wa_bf[e][u].rearrange("p (v m j) -> p m j v", v=2, j=PACK)[:, m0:m1]
             copy(dst, src)
 
         def quantise_wa(e, u):
             cols = slice(2 * u * P, (2 * u + 2) * P)
-            nc.vector.quantize_mx(
-                out=wa_codes[e][:, cols].bitcast(FP8X4),
-                scales=wa_scale[e][:, cols],
-                in_=wa_bf[u],
-            )
+            nc.vector.quantize_mx(out=wa_codes[e][:, cols].bitcast(FP8X4), scales=wa_scale[e][:, cols], in_=wa_bf[e][u])
 
         def round_wb(e, c0, c1, copy):
             src = wb_raw[e][:].rearrange("p j (c i) -> p c j i", i=4)[:, c0:c1]
-            dst = wb_bf[e].rearrange("p (c i j) -> p c j i", i=4, j=PACK)[:, c0:c1]
+            dst = wb_bf[e][:].rearrange("p (c i j) -> p c j i", i=4, j=PACK)[:, c0:c1]
             copy(dst, src)
 
-        def quantise_wb(e):
+        def quantise(codes, scale, values, first, count):
             nc.vector.quantize_mx(
-                out=wb_codes[e][:].bitcast(FP8X4),
-                scales=wb_scale[e][:],
-                in_=wb_bf[e],
-            )
-
-        def first_layer(e, s):
-            slots = slice(e * C + s * P, e * C + (s + 1) * P)
-            bank = banks[2 * e + s][:].rearrange("p (t s) -> p t s", t=PACK)
-            for t in range(PACK):
-                cols = slice(t * P, (t + 1) * P)
-                nc.tensor.matmul_mx(
-                    bank[:, t, :],
-                    lhsT=wa_codes[e][:, cols].bitcast(FP8X4),
-                    lhsT_scale=wa_scale[e][:, cols],
-                    rhs=gw[:, slots].bitcast(FP8X4),
-                    rhs_scale=gs[:, slots],
-                    start=True,
-                    stop=True,
-                )
-            nc.scalar.activation(h_bf[e][s].rearrange("p (s t) -> p s t", t=PACK), bank.rearrange("p t s -> p s t"), ACT.Relu)
-
-        def quantise_h(e, places, values):
-            nc.vector.quantize_mx(
-                out=h_codes[e][:, places].bitcast(FP8X4),
-                scales=h_scale[e][:, places],
+                out=codes[:, first : first + count].bitcast(FP8X4),
+                scales=scale[:, first : first + count],
                 in_=values,
             )
 
-        def second_layer(e, b, places, acc):
-            cols = slice(b * P, (b + 1) * P)
+        def product(acc, left, left_scale, cols, right, right_scale, moving):
             nc.tensor.matmul_mx(
                 acc,
-                lhsT=wb_codes[e][:, cols].bitcast(FP8X4),
-                lhsT_scale=wb_scale[e][:, cols],
-                rhs=h_codes[e][:, places].bitcast(FP8X4),
-                rhs_scale=h_scale[e][:, places],
+                lhsT=left[:, cols].bitcast(FP8X4),
+                lhsT_scale=left_scale[:, cols],
+                rhs=right[:, moving].bitcast(FP8X4),
+                rhs_scale=right_scale[:, moving],
                 start=True,
                 stop=True,
             )
 
-        def scatter(e, b, first, count, y):
+        def first_layer(e, s, bank):
+            slots = slice(e * C + s * P, e * C + (s + 1) * P)
+            for t in range(PACK):
+                cols = slice(t * P, (t + 1) * P)
+                product(bank[:, cols], wa_codes[e], wa_scale[e], cols, gw, gs, slots)
+
+        def relu(e, s, bank):
+            dst = h_bf[e][s].rearrange("p (s t) -> p s t", t=PACK)
+            nc.scalar.activation(dst, bank[:].rearrange("p (t s) -> p s t", t=PACK), ACT.Relu)
+
+        def second_layer(e, b, first, count, acc):
+            product(acc, wb_codes[e], wb_scale[e], slice(b * P, (b + 1) * P), h_codes[e], h_scale[e], slice(first, first + count))
+
+        def scatter(e, b, first, count, values):
             nc.vector.tensor_tensor(
-                routed[b][:].indirect(listed(e * C + first, count)), y, g[:, e * C + first : e * C + first + count], ALU.mult
+                routed[b][:].indirect(listed(e * C + first, count)), values, g[e][:, first : first + count], ALU.mult
             )
 
-        def base_pieces(b):
-            return ((banks[6 + b][:], slice(0, BANK)), (banks[4][:, b * C : (b + 1) * C], slice(BANK, T)))
+        def frozen_layer(b, tokens, acc):
+            product(acc, ww, ws, slice(b * P, (b + 1) * P), xw, xs, tokens)
 
-        def frozen_layer(b, piece):
-            cols = slice(b * P, (b + 1) * P)
-            acc, tokens = base_pieces(b)[piece]
-            nc.tensor.matmul_mx(
-                acc,
-                lhsT=ww[:, cols].bitcast(FP8X4),
-                lhsT_scale=ws[:, cols],
-                rhs=xw[:, tokens].bitcast(FP8X4),
-                rhs_scale=xs[:, tokens],
-                start=True,
-                stop=True,
-            )
-
-        result = [tile([P, T], F32, "result%d" % b) for b in range(NB)]
-
-        def finish(b, piece):
-            acc, tokens = base_pieces(b)[piece]
+        def finish(b, tokens, acc, queue):
             nc.vector.tensor_tensor(result[b][:, tokens], acc, routed[b][:, tokens], ALU.add)
-
-        def store(queue, b, tokens):
             queue.dma_start(out=out[b * P : (b + 1) * P, tokens], in_=result[b][:, tokens])
 
-        y_tile = tile([P, NB, C], F32, "y_tile")
-        every, lower, upper = slice(0, C), slice(0, P), slice(P, C)
+        nc.vector.memset(xs[:].bitcast(I32), 0)
+        nc.vector.memset(routed[0][:], 0.0)
+        on_scalar(routed[1][:], routed[0][:])
 
         nc.sync.dma_start(offsets[:], offs)
-        load_scales(xs, x_scales)
         nc.sync.dma_start(out=xw[:], in_=x_words[0].rearrange("p t d -> p (t d)").bitcast(I32))
-        load_wa(0)
-        load_wb(0)
-        load_wa(1)
-        nc.sync.dma_start(out=g[:], in_=gate)
-        load_wb(1)
-        gw = tile([P, E * C], I32, "gw")
-        gs = tile([P, E * C], U8, "gs")
-        gather_words(gw[:], 0, E * C)
-        gather_scales(gs[:], 0, E * C)
+        wa_first = wa[0].rearrange("(p j) c -> p j c", j=PACK)
+        nc.sync.dma_start(out=wa_raw[0][:, 0:2, :], in_=wa_first[:, 0:2, :])
+        load_scales(nc.sync, xs, x_scales)
+        nc.sync.dma_start(out=wa_raw[0][:, 2:4, :], in_=wa_first[:, 2:4, :])
+        load_rows(wb_raw[0], wb[0])
+        load_rows(wa_raw[1], wa[1])
+        load_gate(0)
+        load_rows(wb_raw[1], wb[1])
+        load_gate(1)
+        nc.sync.dma_start(out=ww[:], in_=w_words[0].rearrange("p n d -> p (n d)").bitcast(I32))
+        load_scales(nc.sync, ws, w_scales)
+
+        nc.vector.tensor_copy(gw[:].bitcast(U32), xw[:].bitcast(U32).indirect(offsets[:]))
+        nc.vector.tensor_copy(gs[:], xs[:].indirect(offsets[:]))
         round_wa(0, 0, 0, P, on_vector)
         round_wa(0, 1, 0, 40, on_vector)
         round_wa(0, 1, 40, P, on_scalar)
         for u in range(2):
             quantise_wa(0, u)
+        round_wb(0, 0, 32, on_vector)
+        round_wb(0, 32, 64, on_scalar)
+        quantise(wb_codes[0], wb_scale[0], wb_bf[0][:], 0, N)
         for s in range(2):
-            first_layer(0, s)
-        round_wb(0, 0, 64, on_vector)
-        ws = tile([P, N], U8, "ws", tag="wb_raw0")
-        load_scales(ws, w_scales)
-        quantise_wb(0)
-        quantise_h(0, lower, h_bf[0][0])
-        quantise_h(0, upper, h_bf[0][1])
-        second_layer(0, 0, every, banks[2][:, every])
-        second_layer(0, 1, lower, banks[3][:, lower])
-        second_layer(0, 1, upper, banks[4][:, lower])
-        ww = tile([P, N], I32, "ww", tag="h_scale0")
-        nc.sync.dma_start(out=ww[:], in_=w_words[0].rearrange("p n d -> p (n d)").bitcast(I32))
+            first_layer(0, s, banks[s])
+            relu(0, s, banks[s])
+        quantise(h_codes[0], h_scale[0], h_bf[0][0], 0, P)
+        second_layer(0, 0, 0, P, banks[4][:, 0:P])
+        wa_late = tile([P, H * PACK], BF16, "wa_bf1")
+        wa_bf.append([wa_late[:, 0:1024], wa_late[:, 1024:2048]])
         round_wa(1, 0, 0, P, on_vector)
-        round_wa(1, 1, 0, P, on_scalar)
-        for u in range(2):
-            quantise_wa(1, u)
-        y_held = wa_raw[1][:, 0, every]
-        on_scalar(y_held, banks[2][:, every])
-        y_next = wa_raw[1][:, 1, lower]
-        on_scalar(y_next, banks[3][:, lower])
-        scatter(0, 0, 0, C, y_held)
-        scatter(0, 1, 0, P, y_next)
+        quantise(h_codes[0], h_scale[0], h_bf[0][1], P, P)
+        second_layer(0, 0, P, P, banks[5][:, 0:P])
+        second_layer(0, 1, 0, P, banks[5][:, P:C])
+        round_wa(1, 1, 0, 32, on_vector)
+        for m in range(32, P, 48):
+            round_wa(1, 1, m, m + 48, on_scalar)
+        y_first = wa_raw[1][:, 3, C + P : 2 * C]
+        on_scalar(y_first, banks[4][:, 0:P])
+        y_next = wa_raw[1][:, 2, C : 2 * C]
+        on_scalar(y_next, banks[5][:, 0:C])
+        quantise_wa(1, 0)
+        quantise_wa(1, 1)
+        scatter(0, 0, 0, P, y_first)
+        scatter(0, 0, P, P, y_next[:, 0:P])
+        scatter(0, 1, 0, P, y_next[:, P:C])
         round_wb(1, 0, 64, on_scalar)
-        quantise_wb(1)
+        h_last = tile([P, C * PACK], BF16, "h_bf1", tag="wb_raw1")
+        h_bf.append([h_last[:, 0:BANK], h_last[:, BANK : 2 * BANK]])
         for s in range(2):
-            first_layer(1, s)
-        quantise_h(1, every, h_rest[:, 1:3, :].rearrange("p s c -> p (s c)"))
-        y_late = tile([P, P], F32, "y_late", tag="gw")
-        on_scalar(y_late[:], banks[4][:, lower])
-        scatter(0, 1, P, P, y_late[:])
+            first_layer(1, s, banks[2 + s])
+            relu(1, s, banks[2 + s])
+        frozen_layer(0, slice(0, BANK), banks[5][:])
+        quantise(wb_codes[1], wb_scale[1], wb_bf[1][:], 0, N)
+        quantise(h_codes[1], h_scale[1], h_last[:], 0, C)
+        second_layer(0, 1, P, P, banks[2][:, 0:P])
+        on_scalar(y[:, C + P : 2 * C], banks[2][:, 0:P])
+        scatter(0, 1, P, P, y[:, C + P : 2 * C])
         for b in range(NB):
-            second_layer(1, b, every, banks[6 + b][:, every])
-            on_scalar(y_tile[:, b, :], banks[6 + b][:, every])
-            scatter(1, b, 0, C, y_tile[:, b, :])
-        for piece in (1, 0):
-            for b in range(NB):
-                frozen_layer(b, piece)
-        for b in range(NB):
-            finish(b, 0)
-            store(nc.sync, b, slice(0, BANK))
-            finish(b, 1)
-            store(nc.scalar, b, slice(BANK, T))
+            second_layer(1, b, 0, C, banks[b][:, 0:C])
+            on_scalar(y[:, (2 + b) * C : (3 + b) * C], banks[b][:, 0:C])
+        frozen_layer(0, slice(BANK, T), banks[3][:, 0:C])
+        frozen_layer(1, slice(0, BANK), banks[0][:])
+        frozen_layer(1, slice(BANK, T), banks[1][:, 0:C])
+        scatter(1, 0, 0, C, y[:, 2 * C : 3 * C])
+        scatter(1, 1, 0, P, y[:, 3 * C : 3 * C + P])
+        finish(0, slice(0, BANK), banks[5][:], nc.sync)
+        finish(0, slice(BANK, T), banks[3][:, 0:C], nc.scalar)
+        scatter(1, 1, P, P, y[:, 3 * C + P : 4 * C])
+        finish(1, slice(0, BANK), banks[0][:], nc.sync)
+        finish(1, slice(BANK, T), banks[1][:, 0:C], nc.scalar)

@@ -42,28 +42,20 @@ def tile_moe_adp_relu_kernel(
         g = [tile([P, C], F32, "g%d" % e) for e in range(E)]
         wa_raw = [tile([P, PACK, H], F32, "wa_raw%d" % e) for e in range(E)]
         wb_raw = [tile([P, PACK, N], F32, "wb_raw%d" % e) for e in range(E)]
-        wa_bf = [[tile([P, 2 * P * PACK], BF16, "wa_bf0%d" % u)[:] for u in range(2)]]
-        wb_bf = [tile([P, N * PACK], BF16, "wb_bf%d" % e) for e in range(E)]
-        h_first = [tile([P, P * PACK], BF16, "h_bf0%d" % s) for s in range(2)]
-        h_bf = [[h_first[0][:], h_first[1][:]]]
-        wa_codes = [tile([P, H], U32, "wa_codes%d" % e) for e in range(E)]
-        wa_scale = [tile([P, H], U8, "wa_scale%d" % e) for e in range(E)]
-        wb_codes = [tile([P, N], U32, "wb_codes%d" % e) for e in range(E)]
-        wb_scale = [tile([P, N], U8, "wb_scale%d" % e) for e in range(E)]
-        h_codes = [tile([P, C], U32, "h_codes%d" % e) for e in range(E)]
-        h_scale = [tile([P, C], U8, "h_scale%d" % e) for e in range(E)]
-        y = tile([P, E * NB * C], F32, "y")
         routed = [tile([P, T], F32, "routed%d" % b) for b in range(NB)]
         result = [tile([P, T], F32, "result%d" % b) for b in range(NB)]
         banks = [ps.tile([P, BANK], F32, name="bank%d" % i) for i in range(8)]
 
-        def load_scales(queue, plane, rows):
+        def load_scales(plane, rows):
             by_row = rows[0].bitcast(I32).rearrange("(q r) c -> r q c", r=4)
             for r in range(4):
-                queue.dma_start(out=plane[r:P:32, :].bitcast(I32), in_=by_row[r])
+                nc.sync.dma_start(out=plane[r:P:32, :].bitcast(I32), in_=by_row[r])
 
-        def load_rows(raw, matrix):
-            nc.sync.dma_start(out=raw[:], in_=matrix.rearrange("(p j) c -> p j c", j=PACK))
+        def load_rows(raw, matrix, j0=0, j1=PACK):
+            nc.sync.dma_start(out=raw[:, j0:j1, :], in_=matrix.rearrange("(p j) c -> p j c", j=PACK)[:, j0:j1, :])
+
+        def load_words(words, packed):
+            nc.sync.dma_start(out=words[:], in_=packed[0].rearrange("p t d -> p (t d)").bitcast(I32))
 
         def load_gate(e):
             nc.sync.dma_start(out=g[e][:], in_=gate[:, e * C : (e + 1) * C])
@@ -77,136 +69,155 @@ def tile_moe_adp_relu_kernel(
         def on_scalar(dst, src):
             nc.scalar.activation(dst, src, ACT.Copy)
 
-        def round_wa(e, u, m0, m1, copy):
+        def round_wa(e, u, values, m0, m1, copy):
             src = wa_raw[e][:].rearrange("p j (m t) -> p m j t", t=PACK)[:, m0:m1, :, 2 * u : 2 * u + 2]
-            dst = wa_bf[e][u].rearrange("p (v m j) -> p m j v", v=2, j=PACK)[:, m0:m1]
-            copy(dst, src)
+            copy(values.rearrange("p (v m j) -> p m j v", v=2, j=PACK)[:, m0:m1], src)
 
-        def quantise_wa(e, u):
-            cols = slice(2 * u * P, (2 * u + 2) * P)
-            nc.vector.quantize_mx(out=wa_codes[e][:, cols].bitcast(FP8X4), scales=wa_scale[e][:, cols], in_=wa_bf[e][u])
+        def round_wb(e, first, values, copy):
+            count = values.shape[1] // PACK
+            src = wb_raw[e][:, :, first : first + count].rearrange("p j (c i) -> p c j i", i=4)
+            copy(values.rearrange("p (c i j) -> p c j i", i=4, j=PACK), src)
 
-        def round_wb(e, c0, c1, copy):
-            src = wb_raw[e][:].rearrange("p j (c i) -> p c j i", i=4)[:, c0:c1]
-            dst = wb_bf[e][:].rearrange("p (c i j) -> p c j i", i=4, j=PACK)[:, c0:c1]
-            copy(dst, src)
+        def operand(name, width, tag=None, scale_tag=None):
+            return tile([P, width], U32, name + "_codes", tag)[:], tile([P, width], U8, name + "_scale", scale_tag)[:]
 
-        def quantise(codes, scale, values, first, count):
-            nc.vector.quantize_mx(
-                out=codes[:, first : first + count].bitcast(FP8X4),
-                scales=scale[:, first : first + count],
-                in_=values,
-            )
+        def part(op, first, count):
+            return op[0][:, first : first + count], op[1][:, first : first + count]
 
-        def product(acc, left, left_scale, cols, right, right_scale, moving):
+        def quantise(op, values):
+            nc.vector.quantize_mx(out=op[0].bitcast(FP8X4), scales=op[1], in_=values)
+
+        def product(acc, left, right):
             nc.tensor.matmul_mx(
                 acc,
-                lhsT=left[:, cols].bitcast(FP8X4),
-                lhsT_scale=left_scale[:, cols],
-                rhs=right[:, moving].bitcast(FP8X4),
-                rhs_scale=right_scale[:, moving],
+                lhsT=left[0].bitcast(FP8X4),
+                lhsT_scale=left[1],
+                rhs=right[0].bitcast(FP8X4),
+                rhs_scale=right[1],
                 start=True,
                 stop=True,
             )
 
-        def first_layer(e, s, bank):
-            slots = slice(e * C + s * P, e * C + (s + 1) * P)
+        def first_layer(e, s, wa_q, bank):
             for t in range(PACK):
-                cols = slice(t * P, (t + 1) * P)
-                product(bank[:, cols], wa_codes[e], wa_scale[e], cols, gw, gs, slots)
+                product(bank[:, t * P : (t + 1) * P], part(wa_q, t * P, P), part((gw[:], gs[:]), e * C + s * P, P))
 
-        def relu(e, s, bank):
-            dst = h_bf[e][s].rearrange("p (s t) -> p s t", t=PACK)
-            nc.scalar.activation(dst, bank[:].rearrange("p (t s) -> p s t", t=PACK), ACT.Relu)
+        def relu(values, bank):
+            nc.scalar.activation(
+                values.rearrange("p (s t) -> p s t", t=PACK), bank[:].rearrange("p (t s) -> p s t", t=PACK), ACT.Relu
+            )
 
-        def second_layer(e, b, first, count, acc):
-            product(acc, wb_codes[e], wb_scale[e], slice(b * P, (b + 1) * P), h_codes[e], h_scale[e], slice(first, first + count))
-
-        def scatter(e, b, first, count, values):
+        def scatter(e, b, first, values):
+            count = values.shape[1]
             nc.vector.tensor_tensor(
                 routed[b][:].indirect(listed(e * C + first, count)), values, g[e][:, first : first + count], ALU.mult
             )
 
-        def frozen_layer(b, tokens, acc):
-            product(acc, ww, ws, slice(b * P, (b + 1) * P), xw, xs, tokens)
+        def frozen_layer(b, first, acc):
+            product(acc, part((ww[:], ws[:]), b * P, P), part((xw[:], xs[:]), first, acc.shape[1]))
 
-        def finish(b, tokens, acc, queue):
+        def finish(b, first, acc, queue):
+            tokens = slice(first, first + acc.shape[1])
             nc.vector.tensor_tensor(result[b][:, tokens], acc, routed[b][:, tokens], ALU.add)
             queue.dma_start(out=out[b * P : (b + 1) * P, tokens], in_=result[b][:, tokens])
+
+        def bf16(name, width, tag=None):
+            return tile([P, width], BF16, name, tag)[:]
+
+        def f32(name, width, tag=None):
+            return tile([P, width], F32, name, tag)[:]
 
         nc.vector.memset(xs[:].bitcast(I32), 0)
         nc.vector.memset(routed[0][:], 0.0)
         on_scalar(routed[1][:], routed[0][:])
 
         nc.sync.dma_start(offsets[:], offs)
-        nc.sync.dma_start(out=xw[:], in_=x_words[0].rearrange("p t d -> p (t d)").bitcast(I32))
-        wa_first = wa[0].rearrange("(p j) c -> p j c", j=PACK)
-        nc.sync.dma_start(out=wa_raw[0][:, 0:2, :], in_=wa_first[:, 0:2, :])
-        load_scales(nc.sync, xs, x_scales)
-        nc.sync.dma_start(out=wa_raw[0][:, 2:4, :], in_=wa_first[:, 2:4, :])
-        load_rows(wb_raw[0], wb[0])
+        load_words(xw, x_words)
+        load_rows(wa_raw[0], wa[0], 0, 2)
+        load_scales(xs, x_scales)
+        load_rows(wa_raw[0], wa[0], 2, 4)
         load_rows(wa_raw[1], wa[1])
+        load_rows(wb_raw[0], wb[0])
         load_gate(0)
         load_rows(wb_raw[1], wb[1])
         load_gate(1)
-        nc.sync.dma_start(out=ww[:], in_=w_words[0].rearrange("p n d -> p (n d)").bitcast(I32))
-        load_scales(nc.sync, ws, w_scales)
+        load_words(ww, w_words)
+        load_scales(ws, w_scales)
 
         nc.vector.tensor_copy(gw[:].bitcast(U32), xw[:].bitcast(U32).indirect(offsets[:]))
         nc.vector.tensor_copy(gs[:], xs[:].indirect(offsets[:]))
-        round_wa(0, 0, 0, P, on_vector)
-        round_wa(0, 1, 0, 40, on_vector)
-        round_wa(0, 1, 40, P, on_scalar)
+        wa_bf0 = [bf16("wa_bf0%d" % u, 1024) for u in range(2)]
+        round_wa(0, 0, wa_bf0[0], 0, P, on_vector)
+        round_wa(0, 1, wa_bf0[1], 0, 40, on_vector)
+        round_wa(0, 1, wa_bf0[1], 40, P, on_scalar)
+        wa_q0 = operand("wa0", H)
         for u in range(2):
-            quantise_wa(0, u)
-        round_wb(0, 0, 32, on_vector)
-        round_wb(0, 32, 64, on_scalar)
-        quantise(wb_codes[0], wb_scale[0], wb_bf[0][:], 0, N)
+            quantise(part(wa_q0, u * C, C), wa_bf0[u])
+        h_bf00 = bf16("h_bf00", BANK)
         for s in range(2):
-            first_layer(0, s, banks[s])
-            relu(0, s, banks[s])
-        quantise(h_codes[0], h_scale[0], h_bf[0][0], 0, P)
-        second_layer(0, 0, 0, P, banks[4][:, 0:P])
-        wa_late = tile([P, H * PACK], BF16, "wa_bf1")
-        wa_bf.append([wa_late[:, 0:1024], wa_late[:, 1024:2048]])
-        round_wa(1, 0, 0, P, on_vector)
-        quantise(h_codes[0], h_scale[0], h_bf[0][1], P, P)
-        second_layer(0, 0, P, P, banks[5][:, 0:P])
-        second_layer(0, 1, 0, P, banks[5][:, P:C])
-        round_wa(1, 1, 0, 32, on_vector)
-        for m in range(32, P, 48):
-            round_wa(1, 1, m, m + 48, on_scalar)
-        y_first = wa_raw[1][:, 3, C + P : 2 * C]
-        on_scalar(y_first, banks[4][:, 0:P])
-        y_next = wa_raw[1][:, 2, C : 2 * C]
-        on_scalar(y_next, banks[5][:, 0:C])
-        quantise_wa(1, 0)
-        quantise_wa(1, 1)
-        scatter(0, 0, 0, P, y_first)
-        scatter(0, 0, P, P, y_next[:, 0:P])
-        scatter(0, 1, 0, P, y_next[:, P:C])
-        round_wb(1, 0, 64, on_scalar)
-        h_last = tile([P, C * PACK], BF16, "h_bf1", tag="wb_raw1")
-        h_bf.append([h_last[:, 0:BANK], h_last[:, BANK : 2 * BANK]])
+            first_layer(0, s, wa_q0, banks[s])
+        relu(h_bf00, banks[0])
+        wa_bf1 = [bf16("wa_bf1%d" % u, 1024) for u in range(2)]
+        for u in range(2):
+            round_wa(1, u, wa_bf1[u], 0, P, on_vector)
+        wb_bf0 = [bf16("wb_bf0%d" % b, BANK) for b in range(NB)]
+        round_wb(0, 0, wb_bf0[0], on_vector)
+        round_wb(0, P, wb_bf0[1], on_scalar)
+        h_bf01 = bf16("h_bf01", BANK, tag="wb_raw0")
+        relu(h_bf01, banks[1])
+        h_q0 = operand("h0", C, tag="wa_raw1")
+        quantise(part(h_q0, 0, P), h_bf00)
+        wb_q0 = operand("wb0", N)
+        quantise(part(wb_q0, 0, P), wb_bf0[0])
+        product(banks[4][:, 0:P], part(wb_q0, 0, P), part(h_q0, 0, P))
+        wa_q1 = operand("wa1", H, tag="wb_bf00")
+        for u in range(2):
+            quantise(part(wa_q1, u * C, C), wa_bf1[u])
+        quantise(part(h_q0, P, P), h_bf01)
+        product(banks[5][:, 0:P], part(wb_q0, 0, P), part(h_q0, P, P))
+        quantise(part(wb_q0, P, P), wb_bf0[1])
+        y_a = f32("y_a", P)
+        on_scalar(y_a, banks[4][:, 0:P])
+        scatter(0, 0, 0, y_a)
+        wb_bf1 = [bf16("wb_bf1%d" % b, BANK) for b in range(NB)]
+        round_wb(1, 0, wb_bf1[0], on_scalar)
+        y_b = wb_raw[1][:, 0, 0:P]
+        on_scalar(y_b, banks[5][:, 0:P])
+        wb_q1 = operand("wb1", N)
+        quantise(part(wb_q1, 0, P), wb_bf1[0])
+        scatter(0, 0, P, y_b)
+        h_bf1 = [bf16("h_bf1%d" % s, BANK) for s in range(2)]
         for s in range(2):
-            first_layer(1, s, banks[2 + s])
-            relu(1, s, banks[2 + s])
-        frozen_layer(0, slice(0, BANK), banks[5][:])
-        quantise(wb_codes[1], wb_scale[1], wb_bf[1][:], 0, N)
-        quantise(h_codes[1], h_scale[1], h_last[:], 0, C)
-        second_layer(0, 1, P, P, banks[2][:, 0:P])
-        on_scalar(y[:, C + P : 2 * C], banks[2][:, 0:P])
-        scatter(0, 1, P, P, y[:, C + P : 2 * C])
-        for b in range(NB):
-            second_layer(1, b, 0, C, banks[b][:, 0:C])
-            on_scalar(y[:, (2 + b) * C : (3 + b) * C], banks[b][:, 0:C])
-        frozen_layer(0, slice(BANK, T), banks[3][:, 0:C])
-        frozen_layer(1, slice(0, BANK), banks[0][:])
-        frozen_layer(1, slice(BANK, T), banks[1][:, 0:C])
-        scatter(1, 0, 0, C, y[:, 2 * C : 3 * C])
-        scatter(1, 1, 0, P, y[:, 3 * C : 3 * C + P])
-        finish(0, slice(0, BANK), banks[5][:], nc.sync)
-        finish(0, slice(BANK, T), banks[3][:, 0:C], nc.scalar)
-        scatter(1, 1, P, P, y[:, 3 * C + P : 4 * C])
-        finish(1, slice(0, BANK), banks[0][:], nc.sync)
-        finish(1, slice(BANK, T), banks[1][:, 0:C], nc.scalar)
+            first_layer(1, s, wa_q1, banks[2 + s])
+            relu(h_bf1[s], banks[2 + s])
+        product(banks[6][:, 0:P], part(wb_q0, P, P), part(h_q0, 0, P))
+        y_f = f32("y_f", C)
+        on_scalar(y_f[:, 0:P], banks[6][:, 0:P])
+        h_q1 = operand("h1", C)
+        for s in range(2):
+            quantise(part(h_q1, s * P, P), h_bf1[s])
+        scatter(0, 1, 0, y_f[:, 0:P])
+        round_wb(1, P, wb_bf1[1], on_scalar)
+        y_c = f32("y_c", C)
+        for s in range(2):
+            product(banks[s][:, 0:P], part(wb_q1, 0, P), part(h_q1, s * P, P))
+            on_scalar(y_c[:, s * P : (s + 1) * P], banks[s][:, 0:P])
+        scatter(1, 0, 0, y_c[:, 0:P])
+        quantise(part(wb_q1, P, P), wb_bf1[1])
+        scatter(1, 0, P, y_c[:, P:C])
+        product(banks[1][:, 0:P], part(wb_q0, P, P), part(h_q0, P, P))
+        on_scalar(y_f[:, P:C], banks[1][:, 0:P])
+        frozen_layer(0, 0, banks[2][:])
+        frozen_layer(0, BANK, banks[3][:, 0:C])
+        product(banks[3][:, C:BANK], part(wb_q1, P, P), h_q1)
+        y_d = f32("y_d", C)
+        on_scalar(y_d, banks[3][:, C:BANK])
+        frozen_layer(1, 0, banks[0][:])
+        frozen_layer(1, BANK, banks[1][:, 0:C])
+        scatter(0, 1, P, y_f[:, P:C])
+        finish(0, 0, banks[2][:], nc.sync)
+        scatter(1, 1, 0, y_d)
+        finish(0, BANK, banks[3][:, 0:C], nc.scalar)
+        finish(1, 0, banks[0][:, 0:C], nc.sync)
+        finish(1, C, banks[0][:, C:BANK], nc.scalar)
+        finish(1, BANK, banks[1][:, 0:C], nc.sync)

@@ -198,26 +198,30 @@ def tile_moe_adp_relu_kernel(
             quantise(part(h_q1, s * P, P), h_bf1[s])
         scatter(0, 1, 0, y_f[:, 0:P])
         round_wb(1, P, wb_bf1[1], on_scalar)
-        y_c = f32("y_c", C)
-        for s in range(2):
-            product(banks[s][:, 0:P], part(wb_q1, 0, P), part(h_q1, s * P, P))
-            on_scalar(y_c[:, s * P : (s + 1) * P], banks[s][:, 0:P])
-        scatter(1, 0, 0, y_c[:, 0:P])
         quantise(part(wb_q1, P, P), wb_bf1[1])
+        y_c = f32("y_c", C)
+        product(banks[0][:, 0:P], part(wb_q1, 0, P), part(h_q1, 0, P))
+        on_scalar(y_c[:, 0:P], banks[0][:, 0:P])
+        scatter(1, 0, 0, y_c[:, 0:P])
+        product(banks[4][:, 0:C], part(wb_q1, P, P), h_q1)
+        product(banks[4][:, C : C + P], part(wb_q1, 0, P), part(h_q1, P, P))
+        product(banks[0][:, 0:P], part(wb_q0, P, P), part(h_q0, P, P))
+        on_scalar(y_f[:, P:C], banks[0][:, 0:P])
+        scatter(0, 1, P, y_f[:, P:C])
+        on_scalar(y_c[:, P:C], banks[4][:, C : C + P])
+        y_d = f32("y_d", C)
+        nc.vector.tensor_tensor(y_d, banks[4][:, 0:C], g[1][:], ALU.mult)
         scatter(1, 0, P, y_c[:, P:C])
-        product(banks[1][:, 0:P], part(wb_q0, P, P), part(h_q0, P, P))
-        on_scalar(y_f[:, P:C], banks[1][:, 0:P])
         frozen_layer(0, 0, banks[2][:])
         frozen_layer(0, BANK, banks[3][:, 0:C])
-        product(banks[3][:, C:BANK], part(wb_q1, P, P), h_q1)
-        y_d = f32("y_d", C)
-        on_scalar(y_d, banks[3][:, C:BANK])
-        frozen_layer(1, 0, banks[0][:])
+        frozen_layer(1, 0, banks[7][:])
         frozen_layer(1, BANK, banks[1][:, 0:C])
-        scatter(0, 1, P, y_f[:, P:C])
-        finish(0, 0, banks[2][:], nc.sync)
-        scatter(1, 1, 0, y_d)
-        finish(0, BANK, banks[3][:, 0:C], nc.scalar)
-        finish(1, 0, banks[0][:, 0:C], nc.sync)
-        finish(1, C, banks[0][:, C:BANK], nc.scalar)
+        base0 = f32("base0", BANK)
+        on_scalar(base0, banks[2][:])
+        nc.gpsimd.tensor_tensor(result[0][:, 0:BANK], base0, routed[0][:, 0:BANK], ALU.add)
+        nc.scalar.dma_start(out=out[0:P, 0:BANK], in_=result[0][:, 0:BANK])
+        nc.vector.tensor_copy(routed[1][:].indirect(listed(C, C)), y_d)
+        finish(0, BANK, banks[3][:, 0:C], nc.sync)
+        finish(1, 0, banks[7][:, 0:C], nc.sync)
+        finish(1, C, banks[7][:, C:BANK], nc.sync)
         finish(1, BANK, banks[1][:, 0:C], nc.sync)

@@ -39,7 +39,7 @@ def tile_moe_adp_relu_kernel(
         ws = tile([P, N], U8, "ws")
         gw = tile([P, E * C], I32, "gw")
         gs = tile([P, E * C], U8, "gs")
-        g = [tile([P, C], F32, "g%d" % e) for e in range(E)]
+        g = tile([P, E * C], F32, "g")
         wa_raw = [tile([P, PACK, H], F32, "wa_raw%d" % e) for e in range(E)]
         wb_raw = [tile([P, PACK, N], F32, "wb_raw%d" % e) for e in range(E)]
         routed = [tile([P, T], F32, "routed%d" % b) for b in range(NB)]
@@ -58,7 +58,7 @@ def tile_moe_adp_relu_kernel(
             nc.sync.dma_start(out=words[:], in_=packed[0].rearrange("p t d -> p (t d)").bitcast(I32))
 
         def load_gate(e):
-            nc.sync.dma_start(out=g[e][:], in_=gate[:, e * C : (e + 1) * C])
+            nc.sync.dma_start(out=g[:, e * C : (e + 1) * C], in_=gate[:, e * C : (e + 1) * C])
 
         def listed(first, count):
             return offsets[:, first // 16 : (first + count) // 16]
@@ -110,7 +110,7 @@ def tile_moe_adp_relu_kernel(
         def scatter(e, b, first, values):
             count = values.shape[1]
             nc.vector.tensor_tensor(
-                routed[b][:].indirect(listed(e * C + first, count)), values, g[e][:, first : first + count], ALU.mult
+                routed[b][:].indirect(listed(e * C + first, count)), values, g[:, e * C + first : e * C + first + count], ALU.mult
             )
 
         def frozen_layer(b, first, acc):
@@ -120,6 +120,11 @@ def tile_moe_adp_relu_kernel(
             tokens = slice(first, first + acc.shape[1])
             nc.vector.tensor_tensor(result[b][:, tokens], acc, routed[b][:, tokens], ALU.add)
             queue.dma_start(out=out[b * P : (b + 1) * P, tokens], in_=result[b][:, tokens])
+
+        def finish_beside(b, first, base):
+            tokens = slice(first, first + base.shape[1])
+            nc.gpsimd.tensor_tensor(result[b][:, tokens], base, routed[b][:, tokens], ALU.add)
+            nc.scalar.dma_start(out=out[b * P : (b + 1) * P, tokens], in_=result[b][:, tokens])
 
         def bf16(name, width, tag=None):
             return tile([P, width], BF16, name, tag)[:]
@@ -191,7 +196,7 @@ def tile_moe_adp_relu_kernel(
             first_layer(1, s, wa_q1, banks[2 + s])
             relu(h_bf1[s], banks[2 + s])
         product(banks[6][:, 0:P], part(wb_q0, P, P), part(h_q0, 0, P))
-        y_f = f32("y_f", C)
+        y_f = f32("y_f", P)
         on_scalar(y_f[:, 0:P], banks[6][:, 0:P])
         h_q1 = operand("h1", C)
         for s in range(2):
@@ -203,25 +208,25 @@ def tile_moe_adp_relu_kernel(
         product(banks[0][:, 0:P], part(wb_q1, 0, P), part(h_q1, 0, P))
         on_scalar(y_c[:, 0:P], banks[0][:, 0:P])
         scatter(1, 0, 0, y_c[:, 0:P])
-        product(banks[4][:, 0:C], part(wb_q1, P, P), h_q1)
-        product(banks[4][:, C : C + P], part(wb_q1, 0, P), part(h_q1, P, P))
-        product(banks[0][:, 0:P], part(wb_q0, P, P), part(h_q0, P, P))
-        on_scalar(y_f[:, P:C], banks[0][:, 0:P])
-        scatter(0, 1, P, y_f[:, P:C])
-        on_scalar(y_c[:, P:C], banks[4][:, C : C + P])
-        y_d = f32("y_d", C)
-        nc.vector.tensor_tensor(y_d, banks[4][:, 0:C], g[1][:], ALU.mult)
+        product(banks[4][:, 0:P], part(wb_q0, P, P), part(h_q0, P, P))
+        product(banks[4][:, P : 3 * P], part(wb_q1, P, P), h_q1)
+        product(banks[4][:, 3 * P : BANK], part(wb_q1, 0, P), part(h_q1, P, P))
+        on_scalar(y_c[:, P:C], banks[4][:, 3 * P : BANK])
+        y_d = f32("y_d", 3 * P)
+        nc.vector.tensor_tensor(y_d, banks[4][:, 0 : 3 * P], g[:, P : E * C], ALU.mult)
         scatter(1, 0, P, y_c[:, P:C])
         frozen_layer(0, 0, banks[2][:])
         frozen_layer(0, BANK, banks[3][:, 0:C])
         frozen_layer(1, 0, banks[7][:])
         frozen_layer(1, BANK, banks[1][:, 0:C])
-        base0 = f32("base0", BANK)
-        on_scalar(base0, banks[2][:])
-        nc.gpsimd.tensor_tensor(result[0][:, 0:BANK], base0, routed[0][:, 0:BANK], ALU.add)
-        nc.scalar.dma_start(out=out[0:P, 0:BANK], in_=result[0][:, 0:BANK])
-        nc.vector.tensor_copy(routed[1][:].indirect(listed(C, C)), y_d)
-        finish(0, BANK, banks[3][:, 0:C], nc.sync)
+        base0 = f32("base0", T)
+        base1 = f32("base1", C)
+        on_scalar(base0[:, 0:BANK], banks[2][:])
+        on_scalar(base0[:, BANK:T], banks[3][:, 0:C])
+        on_scalar(base1, banks[1][:, 0:C])
+        for first in range(0, T, C):
+            finish_beside(0, first, base0[:, first : first + C])
+        nc.vector.tensor_copy(routed[1][:].indirect(listed(P, 3 * P)), y_d)
         finish(1, 0, banks[7][:, 0:C], nc.sync)
+        finish_beside(1, BANK, base1)
         finish(1, C, banks[7][:, C:BANK], nc.sync)
-        finish(1, BANK, banks[1][:, 0:C], nc.sync)

@@ -19,6 +19,7 @@ P = 128
 PACK = 4
 NB = N // P
 BANK = 512
+SPLIT = 192
 
 
 def tile_moe_adp_relu_kernel(
@@ -107,11 +108,21 @@ def tile_moe_adp_relu_kernel(
                 values.rearrange("p (s t) -> p s t", t=PACK), bank[:].rearrange("p (t s) -> p s t", t=PACK), ACT.Relu
             )
 
-        def scatter(e, b, first, values):
-            count = values.shape[1]
-            nc.vector.tensor_tensor(
-                routed[b][:].indirect(listed(e * C + first, count)), values, g[:, e * C + first : e * C + first + count], ALU.mult
-            )
+        def second_layer(s, wb_q, h_q, bank):
+            for b in range(NB):
+                product(bank[:, b * P : (b + 1) * P], part(wb_q, b * P, P), part(h_q, s * P, P))
+
+        def gate_block(b, first, sums):
+            slots = slice(first, first + sums.shape[1])
+            nc.vector.tensor_tensor(gated[:, b, slots], sums, g[:, slots], ALU.mult)
+
+        def gate_both(first, bank):
+            weights = g[:, first : first + P].unsqueeze(1).to_broadcast([P, NB, P])
+            sums = bank[:, 0 : NB * P].rearrange("p (b s) -> p b s", b=NB)
+            nc.vector.tensor_tensor(gated[:, :, first : first + P], sums, weights, ALU.mult)
+
+        def scatter(b, first, count, copy):
+            copy(routed[b][:].indirect(listed(first, count)), gated[:, b, first : first + count])
 
         def frozen_layer(b, first, acc):
             product(acc, part((ww[:], ws[:]), b * P, P), part((xw[:], xs[:]), first, acc.shape[1]))
@@ -121,16 +132,12 @@ def tile_moe_adp_relu_kernel(
             nc.vector.tensor_tensor(result[b][:, tokens], acc, routed[b][:, tokens], ALU.add)
             queue.dma_start(out=out[b * P : (b + 1) * P, tokens], in_=result[b][:, tokens])
 
-        def finish_beside(b, first, base):
-            tokens = slice(first, first + base.shape[1])
-            nc.gpsimd.tensor_tensor(result[b][:, tokens], base, routed[b][:, tokens], ALU.add)
-            nc.scalar.dma_start(out=out[b * P : (b + 1) * P, tokens], in_=result[b][:, tokens])
-
         def bf16(name, width, tag=None):
             return tile([P, width], BF16, name, tag)[:]
 
         def f32(name, width, tag=None):
             return tile([P, width], F32, name, tag)[:]
+
 
         nc.vector.memset(xs[:].bitcast(I32), 0)
         nc.vector.memset(routed[0][:], 0.0)
@@ -143,8 +150,8 @@ def tile_moe_adp_relu_kernel(
         load_rows(wa_raw[0], wa[0], 2, 4)
         load_rows(wa_raw[1], wa[1])
         load_rows(wb_raw[0], wb[0])
-        load_gate(0)
         load_rows(wb_raw[1], wb[1])
+        load_gate(0)
         load_gate(1)
         load_words(ww, w_words)
         load_scales(ws, w_scales)
@@ -158,75 +165,54 @@ def tile_moe_adp_relu_kernel(
         wa_q0 = operand("wa0", H)
         for u in range(2):
             quantise(part(wa_q0, u * C, C), wa_bf0[u])
-        h_bf00 = bf16("h_bf00", BANK)
+        h_bf0 = bf16("h_bf0", 2 * BANK)
         for s in range(2):
             first_layer(0, s, wa_q0, banks[s])
-        relu(h_bf00, banks[0])
+            relu(h_bf0[:, s * BANK : (s + 1) * BANK], banks[s])
         wa_bf1 = [bf16("wa_bf1%d" % u, 1024) for u in range(2)]
         for u in range(2):
             round_wa(1, u, wa_bf1[u], 0, P, on_vector)
-        wb_bf0 = [bf16("wb_bf0%d" % b, BANK) for b in range(NB)]
-        round_wb(0, 0, wb_bf0[0], on_vector)
-        round_wb(0, P, wb_bf0[1], on_scalar)
-        h_bf01 = bf16("h_bf01", BANK, tag="wb_raw0")
-        relu(h_bf01, banks[1])
-        h_q0 = operand("h0", C, tag="wa_raw1")
-        quantise(part(h_q0, 0, P), h_bf00)
-        wb_q0 = operand("wb0", N)
-        quantise(part(wb_q0, 0, P), wb_bf0[0])
-        product(banks[4][:, 0:P], part(wb_q0, 0, P), part(h_q0, 0, P))
-        wa_q1 = operand("wa1", H, tag="wb_bf00")
+        wa_q1 = operand("wa1", H)
         for u in range(2):
             quantise(part(wa_q1, u * C, C), wa_bf1[u])
-        quantise(part(h_q0, P, P), h_bf01)
-        product(banks[5][:, 0:P], part(wb_q0, 0, P), part(h_q0, P, P))
-        quantise(part(wb_q0, P, P), wb_bf0[1])
-        y_a = f32("y_a", P)
-        on_scalar(y_a, banks[4][:, 0:P])
-        scatter(0, 0, 0, y_a)
-        wb_bf1 = [bf16("wb_bf1%d" % b, BANK) for b in range(NB)]
-        round_wb(1, 0, wb_bf1[0], on_scalar)
-        y_b = wb_raw[1][:, 0, 0:P]
-        on_scalar(y_b, banks[5][:, 0:P])
-        wb_q1 = operand("wb1", N)
-        quantise(part(wb_q1, 0, P), wb_bf1[0])
-        scatter(0, 0, P, y_b)
+        wb_bf0 = [bf16("wb_bf0%d" % b, BANK) for b in range(NB)]
+        round_wb(0, P, wb_bf0[1], on_scalar)
+        round_wb(0, 0, wb_bf0[0], on_vector)
         h_bf1 = [bf16("h_bf1%d" % s, BANK) for s in range(2)]
         for s in range(2):
             first_layer(1, s, wa_q1, banks[2 + s])
             relu(h_bf1[s], banks[2 + s])
-        product(banks[6][:, 0:P], part(wb_q0, P, P), part(h_q0, 0, P))
-        y_f = f32("y_f", P)
-        on_scalar(y_f[:, 0:P], banks[6][:, 0:P])
+        h_q0 = operand("h0", C, tag="wa_bf11")
+        quantise(h_q0, h_bf0)
+        wb_q0 = operand("wb0", N)
+        quantise(part(wb_q0, 0, P), wb_bf0[0])
+        quantise(part(wb_q0, P, P), wb_bf0[1])
+        wb_bf1 = bf16("wb_bf1", 2 * BANK)
+        round_wb(1, 0, wb_bf1, on_vector)
+        gated = tile([P, NB, E * C], F32, "gated", tag="wb_raw1")
+        for b in range(NB):
+            product(banks[6 + b][:, 0:C], part(wb_q0, b * P, P), h_q0)
+        gate_block(0, 0, banks[6][:, 0:C])
+        scatter(0, 0, SPLIT, on_scalar)
+        wb_q1 = operand("wb1", N)
         h_q1 = operand("h1", C)
-        for s in range(2):
-            quantise(part(h_q1, s * P, P), h_bf1[s])
-        scatter(0, 1, 0, y_f[:, 0:P])
-        round_wb(1, P, wb_bf1[1], on_scalar)
-        quantise(part(wb_q1, P, P), wb_bf1[1])
-        y_c = f32("y_c", C)
-        product(banks[0][:, 0:P], part(wb_q1, 0, P), part(h_q1, 0, P))
-        on_scalar(y_c[:, 0:P], banks[0][:, 0:P])
-        scatter(1, 0, 0, y_c[:, 0:P])
-        product(banks[4][:, 0:P], part(wb_q0, P, P), part(h_q0, P, P))
-        product(banks[4][:, P : 3 * P], part(wb_q1, P, P), h_q1)
-        product(banks[4][:, 3 * P : BANK], part(wb_q1, 0, P), part(h_q1, P, P))
-        on_scalar(y_c[:, P:C], banks[4][:, 3 * P : BANK])
-        y_d = f32("y_d", 3 * P)
-        nc.vector.tensor_tensor(y_d, banks[4][:, 0 : 3 * P], g[:, P : E * C], ALU.mult)
-        scatter(1, 0, P, y_c[:, P:C])
-        frozen_layer(0, 0, banks[2][:])
-        frozen_layer(0, BANK, banks[3][:, 0:C])
-        frozen_layer(1, 0, banks[7][:])
-        frozen_layer(1, BANK, banks[1][:, 0:C])
-        base0 = f32("base0", T)
-        base1 = f32("base1", C)
-        on_scalar(base0[:, 0:BANK], banks[2][:])
-        on_scalar(base0[:, BANK:T], banks[3][:, 0:C])
-        on_scalar(base1, banks[1][:, 0:C])
-        for first in range(0, T, C):
-            finish_beside(0, first, base0[:, first : first + C])
-        nc.vector.tensor_copy(routed[1][:].indirect(listed(P, 3 * P)), y_d)
-        finish(1, 0, banks[7][:, 0:C], nc.sync)
-        finish_beside(1, BANK, base1)
-        finish(1, C, banks[7][:, C:BANK], nc.sync)
+        quantise(wb_q1, wb_bf1)
+        quantise(part(h_q1, 0, P), h_bf1[0])
+        second_layer(0, wb_q1, h_q1, banks[4])
+        gate_block(1, 0, banks[7][:, 0:C])
+        scatter(1, 0, C, on_scalar)
+        quantise(part(h_q1, P, P), h_bf1[1])
+        second_layer(1, wb_q1, h_q1, banks[5])
+        gate_both(C, banks[4])
+        gate_both(C + P, banks[5])
+        scatter(0, SPLIT, E * C - SPLIT, on_vector)
+        scatter(1, C, C, on_scalar)
+        frozen_layer(0, 0, banks[0][:])
+        frozen_layer(0, BANK, banks[6][:, 0:C])
+        frozen_layer(1, 0, banks[1][:])
+        frozen_layer(1, BANK, banks[7][:, 0:C])
+        finish(0, 0, banks[0][:], nc.sync)
+        finish(0, BANK, banks[6][:, 0:C], nc.sync)
+        finish(1, 0, banks[1][:, 0:C], nc.sync)
+        finish(1, C, banks[1][:, C:BANK], nc.sync)
+        finish(1, BANK, banks[7][:, 0:C], nc.sync)

@@ -38,11 +38,10 @@ def tile_moe_adp_relu_kernel(
         xs = tile([P, T], U8, "xs")
         ww = tile([P, N], I32, "ww")
         ws = tile([P, N], U8, "ws")
-        gw = tile([P, E * C], I32, "gw")
         gs = tile([P, E * C], U8, "gs")
         g = tile([P, E * C], F32, "g")
-        wa_raw = [tile([P, PACK, H], F32, "wa_raw%d" % e) for e in range(E)]
-        wb_raw = [tile([P, PACK, N], F32, "wb_raw%d" % e) for e in range(E)]
+        wa_raw = [tile([P, PACK * H], F32, "wa_raw%d" % e) for e in range(E)]
+        wb_raw = [tile([P, PACK * N], F32, "wb_raw%d" % e) for e in range(E)]
         routed = [tile([P, T], F32, "routed%d" % b) for b in range(NB)]
         result = [tile([P, T], F32, "result%d" % b) for b in range(NB)]
         banks = [ps.tile([P, BANK], F32, name="bank%d" % i) for i in range(8)]
@@ -53,7 +52,8 @@ def tile_moe_adp_relu_kernel(
                 nc.sync.dma_start(out=plane[r:P:32, :].bitcast(I32), in_=by_row[r])
 
         def load_rows(raw, matrix, j0=0, j1=PACK):
-            nc.sync.dma_start(out=raw[:, j0:j1, :], in_=matrix.rearrange("(p j) c -> p j c", j=PACK)[:, j0:j1, :])
+            run = slice(j0 * matrix.shape[1], j1 * matrix.shape[1])
+            nc.sync.dma_start(out=raw[:, run], in_=matrix.rearrange("(p j) c -> p (j c)", j=PACK)[:, run])
 
         def load_words(words, packed):
             nc.sync.dma_start(out=words[:], in_=packed[0].rearrange("p t d -> p (t d)").bitcast(I32))
@@ -64,19 +64,22 @@ def tile_moe_adp_relu_kernel(
         def listed(first, count):
             return offsets[:, first // 16 : (first + count) // 16]
 
+        def gather_words(words, first):
+            nc.vector.tensor_copy(words.bitcast(U32), xw[:].bitcast(U32).indirect(listed(first, words.shape[1])))
+
         def on_vector(dst, src):
             nc.vector.tensor_copy(dst, src)
 
         def on_scalar(dst, src):
             nc.scalar.activation(dst, src, ACT.Copy)
 
-        def round_wa(e, u, values, m0, m1, copy):
-            src = wa_raw[e][:].rearrange("p j (m t) -> p m j t", t=PACK)[:, m0:m1, :, 2 * u : 2 * u + 2]
-            copy(values.rearrange("p (v m j) -> p m j v", v=2, j=PACK)[:, m0:m1], src)
+        def round_wa(e, u, values, copy, j0=0, j1=PACK, m0=0, m1=P):
+            src = wa_raw[e][:, j0 * H : j1 * H].rearrange("p (j m t) -> p m j t", m=P, t=PACK)[:, m0:m1, :, 2 * u : 2 * u + 2]
+            copy(values.rearrange("p (v m j) -> p m j v", v=2, j=PACK)[:, m0:m1, j0:j1], src)
 
         def round_wb(e, first, values, copy):
             count = values.shape[1] // PACK
-            src = wb_raw[e][:, :, first : first + count].rearrange("p j (c i) -> p c j i", i=4)
+            src = wb_raw[e][:].rearrange("p (j c) -> p j c", j=PACK)[:, :, first : first + count].rearrange("p j (c i) -> p c j i", i=4)
             copy(values.rearrange("p (c i j) -> p c j i", i=4, j=PACK), src)
 
         def operand(name, width, tag=None, scale_tag=None):
@@ -99,9 +102,9 @@ def tile_moe_adp_relu_kernel(
                 stop=True,
             )
 
-        def first_layer(e, s, wa_q, bank):
+        def first_layer(first, words, wa_q, bank):
             for t in range(PACK):
-                product(bank[:, t * P : (t + 1) * P], part(wa_q, t * P, P), part((gw[:], gs[:]), e * C + s * P, P))
+                product(bank[:, t * P : (t + 1) * P], part(wa_q, t * P, P), (words, gs[:, first : first + P]))
 
         def relu(values, bank):
             nc.scalar.activation(
@@ -144,10 +147,10 @@ def tile_moe_adp_relu_kernel(
         on_scalar(routed[1][:], routed[0][:])
 
         nc.sync.dma_start(offsets[:], offs)
-        load_words(xw, x_words)
         load_rows(wa_raw[0], wa[0], 0, 2)
         load_scales(xs, x_scales)
         load_rows(wa_raw[0], wa[0], 2, 4)
+        load_words(xw, x_words)
         load_rows(wa_raw[1], wa[1])
         load_rows(wb_raw[0], wb[0])
         load_rows(wb_raw[1], wb[1])
@@ -156,31 +159,35 @@ def tile_moe_adp_relu_kernel(
         load_words(ww, w_words)
         load_scales(ws, w_scales)
 
-        nc.vector.tensor_copy(gw[:].bitcast(U32), xw[:].bitcast(U32).indirect(offsets[:]))
         nc.vector.tensor_copy(gs[:], xs[:].indirect(offsets[:]))
         wa_bf0 = [bf16("wa_bf0%d" % u, 1024) for u in range(2)]
-        round_wa(0, 0, wa_bf0[0], 0, P, on_vector)
-        round_wa(0, 1, wa_bf0[1], 0, 40, on_vector)
-        round_wa(0, 1, wa_bf0[1], 40, P, on_scalar)
+        round_wa(0, 0, wa_bf0[0], on_vector)
+        round_wa(0, 1, wa_bf0[1], on_scalar)
         wa_q0 = operand("wa0", H)
+        gw_first = tile([P, P], I32, "gw_first")
+        gather_words(gw_first[:], 0)
         for u in range(2):
             quantise(part(wa_q0, u * C, C), wa_bf0[u])
+        gw_rest = tile([P, 3 * P], I32, "gw_rest", tag="wa_bf01")
+        gather_words(gw_rest[:, 0:P], P)
+        gather_words(gw_rest[:, P : 3 * P], C)
+        words = [gw_first[:]] + [gw_rest[:, i * P : (i + 1) * P] for i in range(3)]
         h_bf0 = bf16("h_bf0", 2 * BANK)
         for s in range(2):
-            first_layer(0, s, wa_q0, banks[s])
+            first_layer(s * P, words[s], wa_q0, banks[s])
             relu(h_bf0[:, s * BANK : (s + 1) * BANK], banks[s])
         wa_bf1 = [bf16("wa_bf1%d" % u, 1024) for u in range(2)]
         for u in range(2):
-            round_wa(1, u, wa_bf1[u], 0, P, on_vector)
+            round_wa(1, u, wa_bf1[u], on_vector)
         wa_q1 = operand("wa1", H)
         for u in range(2):
             quantise(part(wa_q1, u * C, C), wa_bf1[u])
         wb_bf0 = [bf16("wb_bf0%d" % b, BANK) for b in range(NB)]
+        round_wb(0, 0, wb_bf0[0], on_scalar)
         round_wb(0, P, wb_bf0[1], on_scalar)
-        round_wb(0, 0, wb_bf0[0], on_vector)
         h_bf1 = [bf16("h_bf1%d" % s, BANK) for s in range(2)]
         for s in range(2):
-            first_layer(1, s, wa_q1, banks[2 + s])
+            first_layer(C + s * P, words[2 + s], wa_q1, banks[2 + s])
             relu(h_bf1[s], banks[2 + s])
         h_q0 = operand("h0", C, tag="wa_bf11")
         quantise(h_q0, h_bf0)
@@ -204,15 +211,16 @@ def tile_moe_adp_relu_kernel(
         quantise(part(h_q1, P, P), h_bf1[1])
         second_layer(1, wb_q1, h_q1, banks[5])
         gate_both(C, banks[4])
-        gate_both(C + P, banks[5])
+        gate_block(0, C + P, banks[5][:, 0:P])
+        gate_block(1, C + P, banks[5][:, P:C])
         scatter(0, SPLIT, E * C - SPLIT, on_vector)
         scatter(1, C, C, on_scalar)
         frozen_layer(0, 0, banks[0][:])
         frozen_layer(0, BANK, banks[6][:, 0:C])
         frozen_layer(1, 0, banks[1][:])
         frozen_layer(1, BANK, banks[7][:, 0:C])
-        finish(0, 0, banks[0][:], nc.sync)
         finish(0, BANK, banks[6][:, 0:C], nc.sync)
+        finish(0, 0, banks[0][:], nc.sync)
         finish(1, 0, banks[1][:, 0:C], nc.sync)
         finish(1, C, banks[1][:, C:BANK], nc.sync)
         finish(1, BANK, banks[7][:, 0:C], nc.sync)

@@ -115,17 +115,16 @@ def tile_moe_adp_relu_kernel(
             for b in range(NB):
                 product(bank[:, b * P : (b + 1) * P], part(wb_q, b * P, P), part(h_q, s * P, P))
 
-        def gate_block(b, first, sums):
-            slots = slice(first, first + sums.shape[1])
-            nc.vector.tensor_tensor(gated[:, b, slots], sums, g[:, slots], ALU.mult)
-
-        def gate_both(first, bank):
+        def apply_gate(first, bank, gated):
             weights = g[:, first : first + P].unsqueeze(1).to_broadcast([P, NB, P])
             sums = bank[:, 0 : NB * P].rearrange("p (b s) -> p b s", b=NB)
-            nc.vector.tensor_tensor(gated[:, :, first : first + P], sums, weights, ALU.mult)
+            nc.vector.tensor_tensor(gated, sums, weights, ALU.mult)
 
-        def scatter(b, first, count, copy):
-            copy(routed[b][:].indirect(listed(first, count)), gated[:, b, first : first + count])
+        def gate_block(first, sums, gated):
+            nc.vector.tensor_tensor(gated, sums, g[:, first : first + sums.shape[1]], ALU.mult)
+
+        def scatter(b, first, values, copy):
+            copy(routed[b][:].indirect(listed(first, values.shape[1])), values)
 
         def frozen_layer(b, first, acc):
             product(acc, part((ww[:], ws[:]), b * P, P), part((xw[:], xs[:]), first, acc.shape[1]))
@@ -194,27 +193,28 @@ def tile_moe_adp_relu_kernel(
         wb_q0 = operand("wb0", N)
         quantise(part(wb_q0, 0, P), wb_bf0[0])
         quantise(part(wb_q0, P, P), wb_bf0[1])
-        wb_bf1 = bf16("wb_bf1", 2 * BANK)
-        round_wb(1, 0, wb_bf1, on_vector)
-        gated = tile([P, NB, E * C], F32, "gated", tag="wb_raw1")
         for b in range(NB):
             product(banks[6 + b][:, 0:C], part(wb_q0, b * P, P), h_q0)
-        gate_block(0, 0, banks[6][:, 0:C])
-        scatter(0, 0, SPLIT, on_scalar)
+        wb_bf1 = bf16("wb_bf1", 2 * BANK)
+        round_wb(1, 0, wb_bf1[:, 0:BANK], on_vector)
+        gated = tile([P, NB, E * C], F32, "gated")
+        gate_block(0, banks[6][:, 0:C], gated[:, 0, 0:C])
+        scatter(0, 0, gated[:, 0, 0:SPLIT], on_scalar)
+        round_wb(1, P, wb_bf1[:, BANK : 2 * BANK], on_vector)
         wb_q1 = operand("wb1", N)
         h_q1 = operand("h1", C)
-        quantise(wb_q1, wb_bf1)
         quantise(part(h_q1, 0, P), h_bf1[0])
+        quantise(wb_q1, wb_bf1)
         second_layer(0, wb_q1, h_q1, banks[4])
-        gate_block(1, 0, banks[7][:, 0:C])
-        scatter(1, 0, C, on_scalar)
         quantise(part(h_q1, P, P), h_bf1[1])
         second_layer(1, wb_q1, h_q1, banks[5])
-        gate_both(C, banks[4])
-        gate_block(0, C + P, banks[5][:, 0:P])
-        gate_block(1, C + P, banks[5][:, P:C])
-        scatter(0, SPLIT, E * C - SPLIT, on_vector)
-        scatter(1, C, C, on_scalar)
+        gated01 = f32("gated01", C, tag="wb_raw1")
+        gate_block(0, banks[7][:, 0:C], gated01)
+        scatter(1, 0, gated01, on_scalar)
+        for s in range(2):
+            apply_gate(C + s * P, banks[4 + s], gated[:, :, C + s * P : C + (s + 1) * P])
+        scatter(0, SPLIT, gated[:, 0, SPLIT : E * C], on_vector)
+        scatter(1, C, gated[:, 1, C : E * C], on_scalar)
         frozen_layer(0, 0, banks[0][:])
         frozen_layer(0, BANK, banks[6][:, 0:C])
         frozen_layer(1, 0, banks[1][:])

@@ -19,7 +19,7 @@ P = 128
 PACK = 4
 NB = N // P
 BANK = 512
-SPLIT = 192
+SPLIT = 224
 
 
 def tile_moe_adp_relu_kernel(

@@ -47,9 +47,9 @@ def tile_moe_adp_relu_kernel(
         banks = [ps.tile([P, BANK], F32, name="bank%d" % i) for i in range(8)]
 
         def load_scales(plane, rows):
-            by_row = rows[0].bitcast(I32).rearrange("(q r) c -> r q c", r=4)
-            for r in range(4):
-                nc.sync.dma_start(out=plane[r:P:32, :].bitcast(I32), in_=by_row[r])
+            words = rows[0].bitcast(I32)
+            for q in range(4):
+                nc.sync.dma_start(out=plane[32 * q : 32 * q + 4, :].bitcast(I32), in_=words[4 * q : 4 * q + 4, :])
 
         def load_rows(raw, matrix, j0=0, j1=PACK):
             run = slice(j0 * matrix.shape[1], j1 * matrix.shape[1])
@@ -145,8 +145,8 @@ def tile_moe_adp_relu_kernel(
         nc.vector.memset(routed[0][:], 0.0)
         on_scalar(routed[1][:], routed[0][:])
 
-        nc.sync.dma_start(offsets[:], offs)
         load_rows(wa_raw[0], wa[0], 0, 2)
+        nc.sync.dma_start(offsets[:], offs)
         load_scales(xs, x_scales)
         load_rows(wa_raw[0], wa[0], 2, 4)
         load_words(xw, x_words)

@@ -20,6 +20,7 @@ PACK = 4
 NB = N // P
 BANK = 512
 SPLIT = 224
+AHEAD = 1408
 
 
 def tile_moe_adp_relu_kernel(
@@ -51,8 +52,7 @@ def tile_moe_adp_relu_kernel(
             for q in range(4):
                 nc.sync.dma_start(out=plane[32 * q : 32 * q + 4, :].bitcast(I32), in_=words[4 * q : 4 * q + 4, :])
 
-        def load_rows(raw, matrix, j0=0, j1=PACK):
-            run = slice(j0 * matrix.shape[1], j1 * matrix.shape[1])
+        def load_rows(raw, matrix, run=slice(None)):
             nc.sync.dma_start(out=raw[:, run], in_=matrix.rearrange("(p j) c -> p (j c)", j=PACK)[:, run])
 
         def load_words(words, packed):
@@ -145,10 +145,10 @@ def tile_moe_adp_relu_kernel(
         nc.vector.memset(routed[0][:], 0.0)
         on_scalar(routed[1][:], routed[0][:])
 
-        load_rows(wa_raw[0], wa[0], 0, 2)
+        load_rows(wa_raw[0], wa[0], slice(0, AHEAD))
         nc.sync.dma_start(offsets[:], offs)
         load_scales(xs, x_scales)
-        load_rows(wa_raw[0], wa[0], 2, 4)
+        load_rows(wa_raw[0], wa[0], slice(AHEAD, PACK * H))
         load_words(xw, x_words)
         load_rows(wa_raw[1], wa[1])
         load_rows(wb_raw[0], wb[0])

@@ -20,7 +20,7 @@ PACK = 4
 NB = N // P
 BANK = 512
 SPLIT = 224
-AHEAD = 1408
+AHEAD = 768
 
 
 def tile_moe_adp_relu_kernel(
@@ -188,7 +188,7 @@ def tile_moe_adp_relu_kernel(
         for s in range(2):
             first_layer(C + s * P, words[2 + s], wa_q1, banks[2 + s])
             relu(h_bf1[s], banks[2 + s])
-        h_q0 = operand("h0", C, tag="wa_bf11")
+        h_q0 = operand("h0", C, tag="wa_bf10")
         quantise(h_q0, h_bf0)
         wb_q0 = operand("wb0", N)
         quantise(part(wb_q0, 0, P), wb_bf0[0])

@@ -175,6 +175,8 @@ def tile_moe_adp_relu_kernel(
         for s in range(2):
             first_layer(s * P, words[s], wa_q0, banks[s])
             relu(h_bf0[:, s * BANK : (s + 1) * BANK], banks[s])
+        for first, count in ((0, 256), (256, 128), (384, 64)):
+            product(banks[0][:, first : first + count], part(wa_q0, C, P), part(wa_q0, C, count))
         wa_bf1 = [bf16("wa_bf1%d" % u, 1024) for u in range(2)]
         for u in range(2):
             round_wa(1, u, wa_bf1[u], on_vector)

@@ -154,9 +154,9 @@ def tile_moe_adp_relu_kernel(
         load_rows(wb_raw[0], wb[0])
         load_rows(wb_raw[1], wb[1])
         load_gate(0)
-        load_gate(1)
         load_words(ww, w_words)
         load_scales(ws, w_scales)
+        load_gate(1)
 
         nc.vector.tensor_copy(gs[:], xs[:].indirect(offsets[:]))
         wa_bf0 = [bf16("wa_bf0%d" % u, 1024) for u in range(2)]
@@ -207,6 +207,8 @@ def tile_moe_adp_relu_kernel(
         h_q1 = operand("h1", C)
         quantise(part(h_q1, 0, P), h_bf1[0])
         quantise(wb_q1, wb_bf1)
+        for b in range(NB):
+            frozen_layer(b, BANK, banks[4 + b][:, C:BANK])
         second_layer(0, wb_q1, h_q1, banks[4])
         quantise(part(h_q1, P, P), h_bf1[1])
         second_layer(1, wb_q1, h_q1, banks[5])
@@ -217,12 +219,10 @@ def tile_moe_adp_relu_kernel(
             apply_gate(C + s * P, banks[4 + s], gated[:, :, C + s * P : C + (s + 1) * P])
         scatter(0, SPLIT, gated[:, 0, SPLIT : E * C], on_vector)
         scatter(1, C, gated[:, 1, C : E * C], on_scalar)
-        frozen_layer(0, 0, banks[0][:])
-        frozen_layer(0, BANK, banks[6][:, 0:C])
+        frozen_layer(0, 0, banks[7][:])
         frozen_layer(1, 0, banks[1][:])
-        frozen_layer(1, BANK, banks[7][:, 0:C])
-        finish(0, BANK, banks[6][:, 0:C], nc.sync)
-        finish(0, 0, banks[0][:], nc.sync)
+        finish(0, BANK, banks[4][:, C:BANK], nc.sync)
+        finish(0, 0, banks[7][:], nc.sync)
         finish(1, 0, banks[1][:, 0:C], nc.sync)
         finish(1, C, banks[1][:, C:BANK], nc.sync)
-        finish(1, BANK, banks[7][:, 0:C], nc.sync)
+        finish(1, BANK, banks[5][:, C:BANK], nc.sync)

@@ -31,20 +31,20 @@ def tile_moe_adp_relu_kernel(
         sb = ctx.enter_context(tc.tile_pool(name="sb", bufs=1))
         ps = ctx.enter_context(tc.psum_pool(name="ps", bufs=1))
 
-        def tile(shape, dtype, name, tag=None):
-            return sb.tile(shape, dtype, name=name, tag=tag or name, align_bytes=64)
+        def tile(shape, dtype, name, tag=None, align=64):
+            return sb.tile(shape, dtype, name=name, tag=tag or name, align_bytes=align)
 
         offsets = tile([P, E * C // 16], U16, "offsets")
-        xw = tile([P, T], I32, "xw")
+        xw = tile([P, T], I32, "xw", align=256)
         xs = tile([P, T], U8, "xs")
         ww = tile([P, N], I32, "ww")
         ws = tile([P, N], U8, "ws")
         gs = tile([P, E * C], U8, "gs")
         g = tile([P, E * C], F32, "g")
-        wa_raw = [tile([P, PACK * H], F32, "wa_raw%d" % e) for e in range(E)]
-        wb_raw = [tile([P, PACK * N], F32, "wb_raw%d" % e) for e in range(E)]
+        wa_raw = [tile([P, PACK * H], F32, "wa_raw%d" % e, align=256) for e in range(E)]
+        wb_raw = [tile([P, PACK * N], F32, "wb_raw%d" % e, align=256) for e in range(E)]
         routed = [tile([P, T], F32, "routed%d" % b) for b in range(NB)]
-        result = [tile([P, T], F32, "result%d" % b) for b in range(NB)]
+        result = [tile([P, T], F32, "result%d" % b, align=256) for b in range(NB)]
         banks = [ps.tile([P, BANK], F32, name="bank%d" % i) for i in range(8)]
 
         def load_scales(plane, rows):
@@ -137,9 +137,6 @@ def tile_moe_adp_relu_kernel(
         def bf16(name, width, tag=None):
             return tile([P, width], BF16, name, tag)[:]
 
-        def f32(name, width, tag=None):
-            return tile([P, width], F32, name, tag)[:]
-
 
         nc.vector.memset(xs[:].bitcast(I32), 0)
         nc.vector.memset(routed[0][:], 0.0)
@@ -212,7 +209,7 @@ def tile_moe_adp_relu_kernel(
         second_layer(0, wb_q1, h_q1, banks[4])
         quantise(part(h_q1, P, P), h_bf1[1])
         second_layer(1, wb_q1, h_q1, banks[5])
-        gated01 = f32("gated01", C, tag="wb_raw1")
+        gated01 = tile([P, C], F32, "gated01", tag="wb_raw1", align=256)[:]
         gate_block(0, banks[7][:, 0:C], gated01)
         scatter(1, 0, gated01, on_scalar)
         for s in range(2):

@@ -21,6 +21,8 @@ NB = N // P
 BANK = 512
 SPLIT = 224
 AHEAD = 768
+VECTOR_ROWS = 80
+NARROW = 32
 
 
 def tile_moe_adp_relu_kernel(
@@ -73,9 +75,9 @@ def tile_moe_adp_relu_kernel(
         def on_scalar(dst, src):
             nc.scalar.activation(dst, src, ACT.Copy)
 
-        def round_wa(e, u, values, copy, j0=0, j1=PACK, m0=0, m1=P):
-            src = wa_raw[e][:, j0 * H : j1 * H].rearrange("p (j m t) -> p m j t", m=P, t=PACK)[:, m0:m1, :, 2 * u : 2 * u + 2]
-            copy(values.rearrange("p (v m j) -> p m j v", v=2, j=PACK)[:, m0:m1, j0:j1], src)
+        def round_wa(e, rows, values, copy, runs=slice(None)):
+            src = wa_raw[e][:].rearrange("p (j m t) -> p m j t", j=PACK, t=PACK)[:, rows, :, runs]
+            copy(values.rearrange("p (t m j) -> p m j t", t=PACK, j=PACK)[:, rows, :, runs], src)
 
         def round_wb(e, first, values, copy):
             count = values.shape[1] // PACK
@@ -134,6 +136,9 @@ def tile_moe_adp_relu_kernel(
             nc.vector.tensor_tensor(result[b][:, tokens], acc, routed[b][:, tokens], ALU.add)
             queue.dma_start(out=out[b * P : (b + 1) * P, tokens], in_=result[b][:, tokens])
 
+        def warm_up(left):
+            product(banks[7][0:NARROW, :], left, part((xw[:], xs[:]), 0, BANK))
+
         def bf16(name, width, tag=None):
             return tile([P, width], BF16, name, tag)[:]
 
@@ -156,15 +161,16 @@ def tile_moe_adp_relu_kernel(
         load_gate(1)
 
         nc.vector.tensor_copy(gs[:], xs[:].indirect(offsets[:]))
-        wa_bf0 = [bf16("wa_bf0%d" % u, 1024) for u in range(2)]
-        round_wa(0, 0, wa_bf0[0], on_vector)
-        round_wa(0, 1, wa_bf0[1], on_scalar)
+        wa_bf0 = bf16("wa_bf0", PACK * H)
+        round_wa(0, slice(0, VECTOR_ROWS), wa_bf0, on_vector)
+        round_wa(0, slice(VECTOR_ROWS, P), wa_bf0, on_scalar)
+        warm_up(part((xw[:], xs[:]), 0, NARROW))
         wa_q0 = operand("wa0", H)
         gw_first = tile([P, P], I32, "gw_first")
         gather_words(gw_first[:], 0)
         for u in range(2):
-            quantise(part(wa_q0, u * C, C), wa_bf0[u])
-        gw_rest = tile([P, 3 * P], I32, "gw_rest", tag="wa_bf01")
+            quantise(part(wa_q0, u * C, C), wa_bf0[:, u * 2 * H : (u + 1) * 2 * H])
+        gw_rest = tile([P, 3 * P], I32, "gw_rest", tag="wa_raw0", align=256)
         gather_words(gw_rest[:, 0:P], P)
         gather_words(gw_rest[:, P : 3 * P], C)
         words = [gw_first[:]] + [gw_rest[:, i * P : (i + 1) * P] for i in range(3)]
@@ -172,14 +178,14 @@ def tile_moe_adp_relu_kernel(
         for s in range(2):
             first_layer(s * P, words[s], wa_q0, banks[s])
             relu(h_bf0[:, s * BANK : (s + 1) * BANK], banks[s])
-        for first, count in ((0, 256), (256, 128), (384, 64)):
-            product(banks[0][:, first : first + count], part(wa_q0, C, P), part(wa_q0, C, count))
-        wa_bf1 = [bf16("wa_bf1%d" % u, 1024) for u in range(2)]
+        for i in range(2):
+            warm_up((words[1][:, 0:NARROW], gs[:, P : P + NARROW]))
+        wa_bf1 = bf16("wa_bf1", PACK * H)
         for u in range(2):
-            round_wa(1, u, wa_bf1[u], on_vector)
+            round_wa(1, slice(0, P), wa_bf1, on_vector, slice(2 * u, 2 * u + 2))
         wa_q1 = operand("wa1", H)
         for u in range(2):
-            quantise(part(wa_q1, u * C, C), wa_bf1[u])
+            quantise(part(wa_q1, u * C, C), wa_bf1[:, u * 2 * H : (u + 1) * 2 * H])
         wb_bf0 = [bf16("wb_bf0%d" % b, BANK) for b in range(NB)]
         round_wb(0, 0, wb_bf0[0], on_scalar)
         round_wb(0, P, wb_bf0[1], on_scalar)
@@ -187,7 +193,7 @@ def tile_moe_adp_relu_kernel(
         for s in range(2):
             first_layer(C + s * P, words[2 + s], wa_q1, banks[2 + s])
             relu(h_bf1[s], banks[2 + s])
-        h_q0 = operand("h0", C, tag="wa_bf10")
+        h_q0 = tile([P, C], U32, "h0_codes", tag="wa_raw1", align=256)[:], tile([P, C], U8, "h0_scale")[:]
         quantise(h_q0, h_bf0)
         wb_q0 = operand("wb0", N)
         quantise(part(wb_q0, 0, P), wb_bf0[0])

@@ -19,7 +19,7 @@ P = 128
 PACK = 4
 NB = N // P
 BANK = 512
-SPLIT = 224
+SPLIT = 192
 AHEAD = 768
 VECTOR_ROWS = 80
 NARROW = 32

from contextlib import ExitStack

import concourse.mybir as mybir

K, T, E, C, H, N = 512, 768, 2, 256, 512, 256
FLOPS = 2 * K * N * T + 2 * E * C * (K * H + H * N)

F32 = mybir.dt.float32
BF16 = mybir.dt.bfloat16
I32 = mybir.dt.int32
U32 = mybir.dt.uint32
U16 = mybir.dt.uint16
U8 = mybir.dt.uint8
FP8X4 = mybir.dt.float8_e4m3fn_x4
ACT = mybir.ActivationFunctionType
ALU = mybir.AluOpType

P = 128
PACK = 4
NB = N // P
BANK = 512
SPLIT = 192
AHEAD = 768
VECTOR_ROWS = 80
NARROW = 32


def tile_moe_adp_relu_kernel(
    tc, x_words, x_scales, w_words, w_scales, wa, wb, gate, offs, out
):
    nc = tc.nc
    with ExitStack() as ctx:
        sb = ctx.enter_context(tc.tile_pool(name="sb", bufs=1))
        ps = ctx.enter_context(tc.psum_pool(name="ps", bufs=1))

        def tile(shape, dtype, name, tag=None, align=64):
            return sb.tile(shape, dtype, name=name, tag=tag or name, align_bytes=align)

        offsets = tile([P, E * C // 16], U16, "offsets")
        xw = tile([P, T], I32, "xw", align=256)
        xs = tile([P, T], U8, "xs")
        ww = tile([P, N], I32, "ww")
        ws = tile([P, N], U8, "ws")
        gs = tile([P, E * C], U8, "gs")
        g = tile([P, E * C], F32, "g")
        wa_raw = [tile([P, PACK * H], F32, "wa_raw%d" % e, align=256) for e in range(E)]
        wb_raw = [tile([P, PACK * N], F32, "wb_raw%d" % e, align=256) for e in range(E)]
        routed = [tile([P, T], F32, "routed%d" % b) for b in range(NB)]
        result = [tile([P, T], F32, "result%d" % b, align=256) for b in range(NB)]
        banks = [ps.tile([P, BANK], F32, name="bank%d" % i) for i in range(8)]

        def load_scales(plane, rows):
            words = rows[0].bitcast(I32)
            for q in range(4):
                nc.sync.dma_start(out=plane[32 * q : 32 * q + 4, :].bitcast(I32), in_=words[4 * q : 4 * q + 4, :])

        def load_rows(raw, matrix, run=slice(None)):
            nc.sync.dma_start(out=raw[:, run], in_=matrix.rearrange("(p j) c -> p (j c)", j=PACK)[:, run])

        def load_words(words, packed):
            nc.sync.dma_start(out=words[:], in_=packed[0].rearrange("p t d -> p (t d)").bitcast(I32))

        def load_gate(e):
            nc.sync.dma_start(out=g[:, e * C : (e + 1) * C], in_=gate[:, e * C : (e + 1) * C])

        def listed(first, count):
            return offsets[:, first // 16 : (first + count) // 16]

        def gather_words(words, first):
            nc.vector.tensor_copy(words.bitcast(U32), xw[:].bitcast(U32).indirect(listed(first, words.shape[1])))

        def on_vector(dst, src):
            nc.vector.tensor_copy(dst, src)

        def on_scalar(dst, src):
            nc.scalar.activation(dst, src, ACT.Copy)

        def round_wa(e, rows, values, copy, runs=slice(None)):
            src = wa_raw[e][:].rearrange("p (j m t) -> p m j t", j=PACK, t=PACK)[:, rows, :, runs]
            copy(values.rearrange("p (t m j) -> p m j t", t=PACK, j=PACK)[:, rows, :, runs], src)

        def round_wb(e, first, values, copy):
            count = values.shape[1] // PACK
            src = wb_raw[e][:].rearrange("p (j c) -> p j c", j=PACK)[:, :, first : first + count].rearrange("p j (c i) -> p c j i", i=4)
            copy(values.rearrange("p (c i j) -> p c j i", i=4, j=PACK), src)

        def operand(name, width, tag=None, scale_tag=None):
            return tile([P, width], U32, name + "_codes", tag)[:], tile([P, width], U8, name + "_scale", scale_tag)[:]

        def part(op, first, count):
            return op[0][:, first : first + count], op[1][:, first : first + count]

        def quantise(op, values):
            nc.vector.quantize_mx(out=op[0].bitcast(FP8X4), scales=op[1], in_=values)

        def product(acc, left, right):
            nc.tensor.matmul_mx(
                acc,
                lhsT=left[0].bitcast(FP8X4),
                lhsT_scale=left[1],
                rhs=right[0].bitcast(FP8X4),
                rhs_scale=right[1],
                start=True,
                stop=True,
            )

        def first_layer(first, words, wa_q, bank):
            for t in range(PACK):
                product(bank[:, t * P : (t + 1) * P], part(wa_q, t * P, P), (words, gs[:, first : first + P]))

        def relu(values, bank):
            nc.scalar.activation(
                values.rearrange("p (s t) -> p s t", t=PACK), bank[:].rearrange("p (t s) -> p s t", t=PACK), ACT.Relu
            )

        def second_layer(s, wb_q, h_q, bank):
            for b in range(NB):
                product(bank[:, b * P : (b + 1) * P], part(wb_q, b * P, P), part(h_q, s * P, P))

        def apply_gate(first, bank, gated):
            weights = g[:, first : first + P].unsqueeze(1).to_broadcast([P, NB, P])
            sums = bank[:, 0 : NB * P].rearrange("p (b s) -> p b s", b=NB)
            nc.vector.tensor_tensor(gated, sums, weights, ALU.mult)

        def gate_block(first, sums, gated):
            nc.vector.tensor_tensor(gated, sums, g[:, first : first + sums.shape[1]], ALU.mult)

        def scatter(b, first, values, copy):
            copy(routed[b][:].indirect(listed(first, values.shape[1])), values)

        def frozen_layer(b, first, acc):
            product(acc, part((ww[:], ws[:]), b * P, P), part((xw[:], xs[:]), first, acc.shape[1]))

        def finish(b, first, acc, queue):
            tokens = slice(first, first + acc.shape[1])
            nc.vector.tensor_tensor(result[b][:, tokens], acc, routed[b][:, tokens], ALU.add)
            queue.dma_start(out=out[b * P : (b + 1) * P, tokens], in_=result[b][:, tokens])

        def warm_up(left):
            product(banks[7][0:NARROW, :], left, part((xw[:], xs[:]), 0, BANK))

        def bf16(name, width, tag=None):
            return tile([P, width], BF16, name, tag)[:]


        nc.vector.memset(xs[:].bitcast(I32), 0)
        nc.vector.memset(routed[0][:], 0.0)
        on_scalar(routed[1][:], routed[0][:])

        load_rows(wa_raw[0], wa[0], slice(0, AHEAD))
        nc.sync.dma_start(offsets[:], offs)
        load_scales(xs, x_scales)
        load_rows(wa_raw[0], wa[0], slice(AHEAD, PACK * H))
        load_words(xw, x_words)
        load_rows(wa_raw[1], wa[1])
        load_rows(wb_raw[0], wb[0])
        load_rows(wb_raw[1], wb[1])
        load_gate(0)
        load_words(ww, w_words)
        load_scales(ws, w_scales)
        load_gate(1)

        nc.vector.tensor_copy(gs[:], xs[:].indirect(offsets[:]))
        wa_bf0 = bf16("wa_bf0", PACK * H)
        round_wa(0, slice(0, VECTOR_ROWS), wa_bf0, on_vector)
        round_wa(0, slice(VECTOR_ROWS, P), wa_bf0, on_scalar)
        warm_up(part((xw[:], xs[:]), 0, NARROW))
        wa_q0 = operand("wa0", H)
        gw_first = tile([P, P], I32, "gw_first")
        gather_words(gw_first[:], 0)
        for u in range(2):
            quantise(part(wa_q0, u * C, C), wa_bf0[:, u * 2 * H : (u + 1) * 2 * H])
        gw_rest = tile([P, 3 * P], I32, "gw_rest", tag="wa_raw0", align=256)
        gather_words(gw_rest[:, 0:P], P)
        gather_words(gw_rest[:, P : 3 * P], C)
        words = [gw_first[:]] + [gw_rest[:, i * P : (i + 1) * P] for i in range(3)]
        h_bf0 = bf16("h_bf0", 2 * BANK)
        for s in range(2):
            first_layer(s * P, words[s], wa_q0, banks[s])
            relu(h_bf0[:, s * BANK : (s + 1) * BANK], banks[s])
        for i in range(2):
            warm_up((words[1][:, 0:NARROW], gs[:, P : P + NARROW]))
        wa_bf1 = bf16("wa_bf1", PACK * H)
        for u in range(2):
            round_wa(1, slice(0, P), wa_bf1, on_vector, slice(2 * u, 2 * u + 2))
        wa_q1 = operand("wa1", H)
        for u in range(2):
            quantise(part(wa_q1, u * C, C), wa_bf1[:, u * 2 * H : (u + 1) * 2 * H])
        wb_bf0 = [bf16("wb_bf0%d" % b, BANK) for b in range(NB)]
        round_wb(0, 0, wb_bf0[0], on_scalar)
        round_wb(0, P, wb_bf0[1], on_scalar)
        h_bf1 = [bf16("h_bf1%d" % s, BANK) for s in range(2)]
        for s in range(2):
            first_layer(C + s * P, words[2 + s], wa_q1, banks[2 + s])
            relu(h_bf1[s], banks[2 + s])
        h_q0 = tile([P, C], U32, "h0_codes", tag="wa_raw1", align=256)[:], tile([P, C], U8, "h0_scale")[:]
        quantise(h_q0, h_bf0)
        wb_q0 = operand("wb0", N)
        quantise(part(wb_q0, 0, P), wb_bf0[0])
        quantise(part(wb_q0, P, P), wb_bf0[1])
        for b in range(NB):
            product(banks[6 + b][:, 0:C], part(wb_q0, b * P, P), h_q0)
        wb_bf1 = bf16("wb_bf1", 2 * BANK)
        round_wb(1, 0, wb_bf1[:, 0:BANK], on_vector)
        gated = tile([P, NB, E * C], F32, "gated")
        gate_block(0, banks[6][:, 0:C], gated[:, 0, 0:C])
        scatter(0, 0, gated[:, 0, 0:SPLIT], on_scalar)
        round_wb(1, P, wb_bf1[:, BANK : 2 * BANK], on_vector)
        wb_q1 = operand("wb1", N)
        h_q1 = operand("h1", C)
        quantise(part(h_q1, 0, P), h_bf1[0])
        quantise(wb_q1, wb_bf1)
        for b in range(NB):
            frozen_layer(b, BANK, banks[4 + b][:, C:BANK])
        second_layer(0, wb_q1, h_q1, banks[4])
        quantise(part(h_q1, P, P), h_bf1[1])
        second_layer(1, wb_q1, h_q1, banks[5])
        gated01 = tile([P, C], F32, "gated01", tag="wb_raw1", align=256)[:]
        gate_block(0, banks[7][:, 0:C], gated01)
        scatter(1, 0, gated01, on_scalar)
        for s in range(2):
            apply_gate(C + s * P, banks[4 + s], gated[:, :, C + s * P : C + (s + 1) * P])
        scatter(0, SPLIT, gated[:, 0, SPLIT : E * C], on_vector)
        scatter(1, C, gated[:, 1, C : E * C], on_scalar)
        frozen_layer(0, 0, banks[7][:])
        frozen_layer(1, 0, banks[1][:])
        finish(0, BANK, banks[4][:, C:BANK], nc.sync)
        finish(0, 0, banks[7][:], nc.sync)
        finish(1, 0, banks[1][:, 0:C], nc.sync)
        finish(1, C, banks[1][:, C:BANK], nc.sync)
        finish(1, BANK, banks[5][:, C:BANK], nc.sync)
